import numpy as np
import ml_dtypes


def mxq(x, axis, fmt="e4m3"):
    dtype, down = {"e4m3": (ml_dtypes.float8_e4m3fn, 7), "e5m2": (ml_dtypes.float8_e5m2, 14)}[fmt]
    v = np.moveaxis(np.asarray(x, np.float32).astype(ml_dtypes.bfloat16).astype(np.float64), axis, -1)
    blocks = v.reshape(v.shape[:-1] + (-1, 32))
    amax = np.abs(blocks).max(-1, keepdims=True)
    byte = np.maximum(np.where(amax > 0, np.frexp(amax)[1] - 1 + 127, 0) - down, 1)
    scale = np.exp2(byte - 127.0)
    codes = (blocks / scale).astype(np.float32).astype(dtype).astype(np.float64)
    return np.moveaxis((codes * scale).reshape(v.shape), -1, axis)


WIDE = False


def mx_kscale(k):
    if not WIDE:
        return np.ones(k)
    levels = np.array([10, -10, 5, -5, 0])
    if k % 512:
        return np.exp2(np.random.permutation(np.resize(levels, k // 32))).repeat(32)
    a = np.empty((k // 512, 16))
    for p in range(k // 512):
        a[p, :8] = np.random.permutation(np.resize(levels, 8))
        for g in range(8):
            far = levels[np.abs(levels - a[p, g]) >= 10]
            a[p, g + 8] = far[np.random.randint(len(far))]
    return np.exp2(a.ravel()).repeat(32)


def f64(x):
    return np.asarray(x).astype(np.float64)


def striped(idx):
    return np.tile(idx.reshape(-1, 16).T, (8, 1)).astype(np.uint16)


def unstriped(offs):
    return offs[:16].T.reshape(-1).astype(np.int64)


def pack_weight(w):
    k, n = w.shape
    w = f64(np.asarray(w, np.float32).astype(ml_dtypes.bfloat16)).reshape(k // 32, 32, n)
    amax = np.abs(w).max(1)
    byte = np.clip(np.where(amax > 0, np.frexp(amax)[1] - 1 + 127 - 7, 1), 1, 254)
    scaled = (w * np.exp2(127.0 - byte)[:, None, :]).reshape(k, n).astype(np.float32)
    words = np.ascontiguousarray(scaled.reshape(k // 512, 128, 4, n).transpose(0, 1, 3, 2)).astype(ml_dtypes.float8_e4m3fn).view(np.uint8)
    return words, np.ascontiguousarray(byte.astype(np.uint8).reshape(k // 512, 16, n))


def unpack_weight(words, scales):
    g, p, n, _ = words.shape
    vals = np.ascontiguousarray(words).view(ml_dtypes.float8_e4m3fn).astype(np.float64) * np.repeat(np.exp2(scales.astype(np.float64) - 127.0), 8, axis=1)[..., None]
    return vals.transpose(0, 1, 3, 2).reshape(g * 512, n)


E2M1 = np.array([0.0, 0.5, 1.0, 1.5, 2.0, 3.0, 4.0, 6.0, -0.0, -0.5, -1.0, -1.5, -2.0, -3.0, -4.0, -6.0])


def pack_fp4(w):
    k, n = w.shape
    w = f64(np.asarray(w, np.float32).astype(ml_dtypes.bfloat16)).reshape(k // 32, 32, n)
    amax = np.abs(w).max(1)
    mant, ex = np.frexp(amax / 6.0)
    byte = np.clip(np.where(amax > 0, np.where(mant > 0.5, ex, ex - 1) + 127, 1), 1, 254)
    scaled = (w * np.exp2(127.0 - byte)[:, None, :]).reshape(k, n).astype(np.float32)
    c = np.ascontiguousarray(scaled.reshape(k // 512, 128, 4, n).transpose(0, 1, 3, 2)).astype(ml_dtypes.float4_e2m1fn).view(np.uint8) & 0xF
    words = (c[..., 0::2] | (c[..., 1::2] << 4)).reshape(k // 512, 128, 2 * n)
    return np.ascontiguousarray(words), np.ascontiguousarray(byte.astype(np.uint8).reshape(k // 512, 16, n))


def unpack_fp4(words, scales):
    g, _, n = scales.shape
    words = np.ascontiguousarray(words).reshape(g, 128, n, 2)
    nib = np.empty((g, 128, n, 4), np.uint8)
    nib[..., 0::2] = words & 0xF
    nib[..., 1::2] = words >> 4
    vals = E2M1[nib] * np.repeat(np.exp2(scales.astype(np.float64) - 127.0), 8, axis=1)[..., None]
    return vals.transpose(0, 1, 3, 2).reshape(g * 512, n)


K, T, S, V, H, N = 1024, 2048, 1024, 512, 512, 128


def setup_inputs():
    n = np.random.standard_normal
    s = mx_kscale(K)[:, None]
    u = mx_kscale(H)
    packed_xT = pack_weight(n((K, T)) * s)
    packed_w2 = pack_fp4(n((H, N)) / np.sqrt(3 * H) / u[:, None])
    packed_w3 = pack_fp4(n((H, N)) / np.sqrt(3 * H) / u[:, None])
    packed_w4 = pack_fp4(n((H, N)) / np.sqrt(3 * H) / u[:, None])
    return {
        "x_words": packed_xT[0],
        "x_scales": packed_xT[1],
        "w1": (n((K, H)) / np.sqrt(K) / s * u).astype(np.float32),
        "w2_words": packed_w2[0],
        "w2_scales": packed_w2[1],
        "w3_words": packed_w3[0],
        "w3_scales": packed_w3[1],
        "w4_words": packed_w4[0],
        "w4_scales": packed_w4[1],
        "offs": striped(np.random.permutation(T)[:S]),
        "pos1": striped(np.random.permutation(S)[:V]),
        "pos2": striped(np.random.permutation(S)[:V]),
        "pos3": striped(np.random.permutation(S)[:V]),
    }


def reference(x_words, x_scales, w1, w2_words, w2_scales, w3_words, w3_scales, w4_words, w4_scales, offs, pos1, pos2, pos3):
    xq = unpack_weight(x_words, x_scales)[:, unstriped(offs)]
    h = mxq(f64(w1), 0, "e4m3").T @ xq
    g0 = h[:, unstriped(pos1)]
    g1 = h[:, unstriped(pos2)]
    g2 = h[:, unstriped(pos3)]
    z1 = (g0 + g1 + g2) / 3
    z2 = np.maximum(np.maximum(g0, g1), g2)
    z3 = np.minimum(np.minimum(g0, g1), g2)
    return unpack_fp4(w2_words, w2_scales).T @ mxq(z1, 0, "e4m3") + unpack_fp4(w3_words, w3_scales).T @ mxq(z2, 0, "e4m3") + unpack_fp4(w4_words, w4_scales).T @ mxq(z3, 0, "e4m3")

@@ -1,0 +1,242 @@
+from contextlib import ExitStack
+
+import concourse.mybir as mybir
+from concourse.masks import make_identity
+
+K, T, S, V, H, N = 1024, 2048, 1024, 512, 512, 128
+FLOPS = 2 * K * H * S + 3 * 2 * H * N * V
+
+F32 = mybir.dt.float32
+BF16 = mybir.dt.bfloat16
+I32 = mybir.dt.int32
+U32 = mybir.dt.uint32
+U16 = mybir.dt.uint16
+U8 = mybir.dt.uint8
+FP8X4 = mybir.dt.float8_e4m3fn_x4
+FP4X4 = mybir.dt.float4_e2m1fn_x4
+COPY = mybir.ActivationFunctionType.Copy
+MAX = mybir.AluOpType.max
+MIN = mybir.AluOpType.min
+
+P = 128
+PACK = 4
+PASSES = K // (P * PACK)
+BANK = 512
+CHUNK = 256
+SUB = 128
+
+
+def tile_picked_pna_none_p_kernel(
+    tc, x_words, x_scales, w1, w2_words, w2_scales, w3_words, w3_scales, w4_words, w4_scales, offs, pos1, pos2, pos3, out
+):
+    nc = tc.nc
+    with ExitStack() as ctx:
+        lists = ctx.enter_context(tc.tile_pool(name="lists", bufs=1))
+        keep = ctx.enter_context(tc.tile_pool(name="keep", bufs=1))
+        psum = ctx.enter_context(tc.psum_pool(name="psum", bufs=8))
+
+        def bank(name):
+            return psum.tile([P, BANK], F32, name=name, tag="bank")
+
+        offs_sb = lists.tile([P, S // 16], U16, name="offs_sb")
+        pos_sb = [lists.tile([P, V // 16], U16, name=f"pos_sb{d}") for d in range(3)]
+        nc.sync.dma_start(offs_sb[:], offs)
+
+        xs_all = keep.tile([P, T], U8, name="xs_all", align_bytes=64)
+        nc.vector.memset(xs_all[:].bitcast(I32), 0)
+        ws2 = keep.tile([P, 3 * N], U8, name="ws2", align_bytes=64)
+        nc.vector.memset(ws2[:].bitcast(I32), 0)
+        for q in range(4):
+            nc.scalar.dma_start(
+                out=xs_all[32 * q : 32 * q + 8, :].bitcast(I32),
+                in_=x_scales[:, 4 * q : 4 * q + 4, :].bitcast(I32),
+            )
+
+        xw_all = [keep.tile([P, T], I32, name=f"xw_all{z}", align_bytes=64) for z in range(PASSES)]
+        w_rows = [w1[512 * z : 512 * (z + 1), :].rearrange("(p j) c -> p j c", j=PACK) for z in range(PASSES)]
+        w_raw0 = keep.tile([P, PACK, H], F32, name="w_raw0")
+        w_raw1 = [keep.tile([P, PACK, H // 2], F32, name=f"w_raw1{i}") for i in range(2)]
+
+        def load_x(z):
+            nc.sync.dma_start(out=xw_all[z][:], in_=x_words[z].rearrange("p n t -> p (n t)").bitcast(I32))
+
+        load_x(0)
+        nc.sync.dma_start(out=w_raw0[:], in_=w_rows[0])
+        load_x(1)
+        for d, pos in enumerate((pos1, pos2, pos3)):
+            nc.sync.dma_start(pos_sb[d][:], pos)
+        for i in range(2):
+            nc.sync.dma_start(out=w_raw1[i][:], in_=w_rows[1][:, :, 256 * i : 256 * (i + 1)])
+
+        ww2 = [keep.tile([P, 2 * N], U8, name=f"ww2{d}", align_bytes=64) for d in range(3)]
+        for d, (words, scales) in enumerate(((w2_words, w2_scales), (w3_words, w3_scales), (w4_words, w4_scales))):
+            nc.sync.dma_start(out=ww2[d][:].bitcast(I32), in_=words[0].bitcast(I32))
+            for q in range(4):
+                nc.sync.dma_start(
+                    out=ws2[32 * q : 32 * q + 4, d * N : (d + 1) * N].bitcast(I32),
+                    in_=scales[0, 4 * q : 4 * q + 4, :].bitcast(I32),
+                )
+
+        ident = keep.tile([P, P], F32, name="ident")
+        make_identity(nc, ident[:])
+
+        xw = [keep.tile([P, S], U32, name=f"xw{z}", align_bytes=64) for z in range(PASSES)]
+        xs = keep.tile([P, S], U8, name="xs", align_bytes=64)
+        w_bf = [[keep.tile([P, 2, P, PACK], BF16, name=f"w_bf{z}{u}", align_bytes=64) for u in range(2)] for z in range(PASSES)]
+        wq = [keep.tile([P, H], U32, name=f"wq{z}", align_bytes=64) for z in range(PASSES)]
+        wsc = [keep.tile([P, H], U8, name=f"wsc{z}", align_bytes=64) for z in range(PASSES)]
+
+        def w_views(z, u, raw, m0, m1):
+            return (
+                w_bf[z][u][:, :, m0:m1, :].rearrange("p e m j -> p m j e"),
+                raw[:].rearrange("p j (m t) -> p m j t", t=PACK)[:, :, :, 2 * u : 2 * u + 2],
+            )
+
+        def round_w_scalar(*args):
+            dst, src = w_views(*args)
+            nc.scalar.activation(out=dst, in_=src, func=COPY)
+
+        def round_w_vector(*args):
+            dst, src = w_views(*args)
+            nc.vector.tensor_copy(out=dst, in_=src)
+
+        def quantize_w(z, t0, t1):
+            flat = w_bf[z][t0 // 2][:, t0 % 2 : t0 % 2 + t1 - t0, :, :].rearrange("p e m j -> p (e m j)")
+            cols = slice(P * t0, P * t1)
+            nc.vector.quantize_mx(out=wq[z][:, cols].bitcast(FP8X4), scales=wsc[z][:, cols], in_=flat)
+
+        nc.vector.tensor_copy(out=xs[:], in_=xs_all[:].indirect(offs_sb[:]))
+        nc.vector.tensor_copy(out=xw[0][:], in_=xw_all[0][:].bitcast(U32).indirect(offs_sb[:]))
+        round_w_vector(0, 0, w_raw0, 0, P)
+        round_w_scalar(0, 1, w_raw0, 0, P)
+        quantize_w(0, 0, 2)
+        quantize_w(0, 2, 4)
+        nc.vector.tensor_copy(out=xw[1][:], in_=xw_all[1][:].bitcast(U32).indirect(offs_sb[:]))
+        round_w_scalar(1, 0, w_raw1[0], 0, P // 2)
+        round_w_scalar(1, 1, w_raw1[0], 0, P // 2)
+        round_w_vector(1, 0, w_raw1[1], P // 2, P)
+        round_w_scalar(1, 1, w_raw1[1], P // 2, P)
+        quantize_w(1, 0, 1)
+        quantize_w(1, 1, 2)
+        quantize_w(1, 2, 4)
+
+        h = [keep.tile([P, S], F32, name=f"h{t}") for t in range(PACK)]
+        for t in range(PACK):
+            acc = [bank(f"acc{t}{s}") for s in range(2)]
+            for z in range(PASSES):
+                for s in range(2):
+                    cols = slice(BANK * s, BANK * (s + 1))
+                    nc.tensor.matmul_mx(
+                        out=acc[s][:],
+                        lhsT=wq[z][:, P * t : P * (t + 1)].bitcast(FP8X4),
+                        lhsT_scale=wsc[z][:, P * t : P * (t + 1)],
+                        rhs=xw[z][:, cols].bitcast(FP8X4),
+                        rhs_scale=xs[4 * z : P, cols],
+                        start=(z == 0),
+                        stop=(z == PASSES - 1),
+                    )
+            nc.scalar.copy(out=h[t][:, 0:BANK], in_=acc[0][:])
+            if t == 0:
+                nc.vector.tensor_copy(out=h[t][:, BANK:S], in_=acc[1][:])
+            else:
+                nc.scalar.copy(out=h[t][:, BANK:S], in_=acc[1][:])
+
+        n_chunks = V // CHUNK
+        g = []
+
+        def open_chunk(c):
+            g.append([keep.tile([P, PACK, CHUNK], F32, name=f"g{c}{d}", tag=f"g{d}") for d in range(3)])
+
+        gb = [[keep.tile([P, CHUNK * PACK], BF16, name=f"gb{c}{d}", align_bytes=64) for d in range(3)] for c in range(n_chunks)]
+        z1 = [keep.tile([P, CHUNK * PACK], BF16, name=f"z1{c}", align_bytes=64) for c in range(n_chunks)]
+
+        def gather(c, d, t):
+            cols = slice(c * CHUNK // 16, (c + 1) * CHUNK // 16)
+            nc.vector.tensor_copy(out=g[c][d][:, t, :], in_=h[t][:].indirect(pos_sb[d][:, cols]))
+
+        def cast(c, d):
+            nc.scalar.copy(
+                out=gb[c][d][:].rearrange("p (v i t) -> p v t i", i=4, t=PACK),
+                in_=g[c][d][:].rearrange("p t (v i) -> p v t i", i=4),
+            )
+
+        def mean(c):
+            totals = [bank(f"total{c}{s}") for s in range(CHUNK // SUB)]
+            for t in range(PACK):
+                for d in range(3):
+                    for s, total in enumerate(totals):
+                        nc.tensor.matmul(
+                            total[:, P * t : P * (t + 1)],
+                            lhsT=g[c][d][:, t, SUB * s : SUB * (s + 1)],
+                            rhs=ident[:],
+                            is_transpose=True,
+                            start=(d == 0),
+                            stop=(d == 2),
+                        )
+            back = bank(f"back{c}")
+            for s, total in enumerate(totals):
+                turned = keep.tile([P, H], BF16, name=f"turned{c}{s}", align_bytes=64)
+                nc.scalar.activation(
+                    out=turned[:].rearrange("v (u p e) -> v u p e", u=2, e=2),
+                    in_=total[:].rearrange("v (u e p) -> v u p e", u=2, e=2),
+                    func=COPY,
+                    scale=1.0 / 3.0,
+                )
+                pairs = turned[:].bitcast(F32)
+                for u in range(2):
+                    nc.tensor.transpose(back[:, P * (2 * s + u) : P * (2 * s + u + 1)], pairs[:, P * u : P * (u + 1)], ident[:])
+            nc.scalar.copy(
+                out=z1[c][:].bitcast(F32).rearrange("p (s v u) -> p s v u", s=2, u=2),
+                in_=back[:].rearrange("p (s u v) -> p s v u", s=2, u=2),
+            )
+
+        def finish(c):
+            hi = keep.tile([P, CHUNK * PACK], BF16, name=f"hi{c}", align_bytes=64)
+            lo = keep.tile([P, CHUNK * PACK], BF16, name=f"lo{c}", align_bytes=64)
+            z2 = keep.tile([P, CHUNK * PACK], BF16, name=f"z2{c}", align_bytes=64)
+            z3 = keep.tile([P, CHUNK * PACK], BF16, name=f"z3{c}", align_bytes=64)
+            a, b, e = gb[c]
+            nc.vector.tensor_tensor(out=hi[:], in0=a[:], in1=b[:], op=MAX)
+            nc.vector.tensor_tensor(out=lo[:], in0=a[:], in1=b[:], op=MIN)
+            nc.vector.tensor_tensor(out=z2[:], in0=hi[:], in1=e[:], op=MAX)
+            nc.vector.tensor_tensor(out=z3[:], in0=lo[:], in1=e[:], op=MIN)
+            zq = [keep.tile([P, CHUNK], U32, name=f"zq{c}{d}", align_bytes=64) for d in range(3)]
+            zs = [keep.tile([P, CHUNK], U8, name=f"zs{c}{d}", align_bytes=64) for d in range(3)]
+            for d, z in enumerate((z1[c], z2, z3)):
+                nc.vector.quantize_mx(out=zq[d][:].bitcast(FP8X4), scales=zs[d][:], in_=z[:])
+            result = keep.tile([P, CHUNK], F32, name=f"result{c}")
+            res = [bank(f"res{c}{s}") for s in range(CHUNK // SUB)]
+            for d in range(3):
+                for s in range(CHUNK // SUB):
+                    cols = slice(SUB * s, SUB * (s + 1))
+                    nc.tensor.matmul_mx(
+                        out=res[s][:, 0:SUB],
+                        lhsT=ww2[d][:].bitcast(FP4X4),
+                        lhsT_scale=ws2[:, d * N : (d + 1) * N],
+                        rhs=zq[d][:, cols].bitcast(FP8X4),
+                        rhs_scale=zs[d][:, cols],
+                        start=(d == 0),
+                        stop=(d == 2),
+                    )
+            if c == n_chunks - 1:
+                nc.vector.tensor_copy(out=result[:, 0:SUB], in_=res[0][:, 0:SUB])
+            else:
+                nc.scalar.copy(out=result[:, 0:SUB], in_=res[0][:, 0:SUB])
+            nc.scalar.copy(out=result[:, SUB:CHUNK], in_=res[1][:, 0:SUB])
+            nc.sync.dma_start(out=out[:, c * CHUNK : (c + 1) * CHUNK], in_=result[:])
+
+        open_chunk(0)
+        for t in range(PACK):
+            for d in range(3):
+                gather(0, d, t)
+        for d in range(3):
+            cast(0, d)
+        mean(0)
+        open_chunk(1)
+        for d in range(3):
+            for t in range(PACK):
+                gather(1, d, t)
+            cast(1, d)
+        mean(1)
+        finish(0)
+        finish(1)

@@ -33,24 +33,18 @@ def tile_picked_pna_none_p_kernel(
     with ExitStack() as ctx:
         lists = ctx.enter_context(tc.tile_pool(name="lists", bufs=1))
         keep = ctx.enter_context(tc.tile_pool(name="keep", bufs=1))
-        psum = ctx.enter_context(tc.psum_pool(name="psum", bufs=8))
+        psum = ctx.enter_context(tc.psum_pool(name="psum", bufs=1))
 
-        def bank(name):
-            return psum.tile([P, BANK], F32, name=name, tag="bank")
+        def bank(name, index):
+            return psum.tile([P, BANK], F32, name=name, tag=f"bank{index}")
 
         offs_sb = lists.tile([P, S // 16], U16, name="offs_sb")
         pos_sb = [lists.tile([P, V // 16], U16, name=f"pos_sb{d}") for d in range(3)]
-        nc.sync.dma_start(offs_sb[:], offs)
 
         xs_all = keep.tile([P, T], U8, name="xs_all", align_bytes=64)
-        nc.vector.memset(xs_all[:].bitcast(I32), 0)
+        nc.gpsimd.memset(xs_all[:].bitcast(I32), 0)
         ws2 = keep.tile([P, 3 * N], U8, name="ws2", align_bytes=64)
         nc.vector.memset(ws2[:].bitcast(I32), 0)
-        for q in range(4):
-            nc.scalar.dma_start(
-                out=xs_all[32 * q : 32 * q + 8, :].bitcast(I32),
-                in_=x_scales[:, 4 * q : 4 * q + 4, :].bitcast(I32),
-            )
 
         xw_all = [keep.tile([P, T], I32, name=f"xw_all{z}", align_bytes=64) for z in range(PASSES)]
         w_rows = [w1[512 * z : 512 * (z + 1), :].rearrange("(p j) c -> p j c", j=PACK) for z in range(PASSES)]
@@ -61,12 +55,18 @@ def tile_picked_pna_none_p_kernel(
             nc.sync.dma_start(out=xw_all[z][:], in_=x_words[z].rearrange("p n t -> p (n t)").bitcast(I32))
 
         load_x(0)
+        nc.sync.dma_start(offs_sb[:], offs)
+        for q in range(4):
+            nc.sync.dma_start(
+                out=xs_all[32 * q : 32 * q + 8, :].bitcast(I32),
+                in_=x_scales[:, 4 * q : 4 * q + 4, :].bitcast(I32),
+            )
         nc.sync.dma_start(out=w_raw0[:], in_=w_rows[0])
         load_x(1)
-        for d, pos in enumerate((pos1, pos2, pos3)):
-            nc.sync.dma_start(pos_sb[d][:], pos)
         for i in range(2):
             nc.sync.dma_start(out=w_raw1[i][:], in_=w_rows[1][:, :, 256 * i : 256 * (i + 1)])
+        for d, pos in enumerate((pos1, pos2, pos3)):
+            nc.sync.dma_start(pos_sb[d][:], pos)
 
         ww2 = [keep.tile([P, 2 * N], U8, name=f"ww2{d}", align_bytes=64) for d in range(3)]
         for d, (words, scales) in enumerate(((w2_words, w2_scales), (w3_words, w3_scales), (w4_words, w4_scales))):
@@ -79,10 +79,12 @@ def tile_picked_pna_none_p_kernel(
 
         ident = keep.tile([P, P], F32, name="ident")
         make_identity(nc, ident[:])
+        ident_gate = keep.tile([P, P], F32, name="ident_gate", tag="g3")
+        make_identity(nc, ident_gate[:])
 
-        xw = [keep.tile([P, S], U32, name=f"xw{z}", align_bytes=64) for z in range(PASSES)]
+        xw = [keep.tile([P, S], U32, name="xw0", align_bytes=64)]
         xs = keep.tile([P, S], U8, name="xs", align_bytes=64)
-        w_bf = [[keep.tile([P, 2, P, PACK], BF16, name=f"w_bf{z}{u}", align_bytes=64) for u in range(2)] for z in range(PASSES)]
+        w_bf = [[keep.tile([P, 2, P, PACK], BF16, name=f"w_bf{z}{u}", tag=f"w_bf{z}{u}", align_bytes=64) for u in range(2)] for z in range(PASSES)]
         wq = [keep.tile([P, H], U32, name=f"wq{z}", align_bytes=64) for z in range(PASSES)]
         wsc = [keep.tile([P, H], U8, name=f"wsc{z}", align_bytes=64) for z in range(PASSES)]
 
@@ -96,59 +98,72 @@ def tile_picked_pna_none_p_kernel(
             dst, src = w_views(*args)
             nc.scalar.activation(out=dst, in_=src, func=COPY)
 
-        def round_w_vector(*args):
-            dst, src = w_views(*args)
-            nc.vector.tensor_copy(out=dst, in_=src)
-
         def quantize_w(z, t0, t1):
             flat = w_bf[z][t0 // 2][:, t0 % 2 : t0 % 2 + t1 - t0, :, :].rearrange("p e m j -> p (e m j)")
             cols = slice(P * t0, P * t1)
             nc.vector.quantize_mx(out=wq[z][:, cols].bitcast(FP8X4), scales=wsc[z][:, cols], in_=flat)
 
-        nc.vector.tensor_copy(out=xs[:], in_=xs_all[:].indirect(offs_sb[:]))
         nc.vector.tensor_copy(out=xw[0][:], in_=xw_all[0][:].bitcast(U32).indirect(offs_sb[:]))
-        round_w_vector(0, 0, w_raw0, 0, P)
+        nc.vector.tensor_copy(out=xs[:], in_=xs_all[:].indirect(offs_sb[:]))
+        round_w_scalar(0, 0, w_raw0, 0, P)
         round_w_scalar(0, 1, w_raw0, 0, P)
         quantize_w(0, 0, 2)
-        quantize_w(0, 2, 4)
-        nc.vector.tensor_copy(out=xw[1][:], in_=xw_all[1][:].bitcast(U32).indirect(offs_sb[:]))
+        xw1 = []
+        for i in range(2):
+            if i == 1:
+                quantize_w(0, 2, 4)
+            xw1.append(keep.tile([P, BANK], U32, name=f"xw1{i}", tag=f"w_bf0{i}", align_bytes=64))
+            nc.vector.tensor_copy(out=xw1[i][:], in_=xw_all[1][:].bitcast(U32).indirect(offs_sb[:, 32 * i : 32 * (i + 1)]))
+
+        def x_codes(z, c0, c1):
+            if z == 0:
+                return xw[0][:, c0:c1]
+            return xw1[c0 // BANK][:, c0 % BANK : c0 % BANK + c1 - c0]
+
         round_w_scalar(1, 0, w_raw1[0], 0, P // 2)
         round_w_scalar(1, 1, w_raw1[0], 0, P // 2)
-        round_w_vector(1, 0, w_raw1[1], P // 2, P)
+        round_w_scalar(1, 0, w_raw1[1], P // 2, P)
         round_w_scalar(1, 1, w_raw1[1], P // 2, P)
         quantize_w(1, 0, 1)
         quantize_w(1, 1, 2)
         quantize_w(1, 2, 4)
 
-        h = [keep.tile([P, S], F32, name=f"h{t}") for t in range(PACK)]
+        h = [keep.tile([P, S], F32, name=f"h{t}", tag=f"h{t}", align_bytes=64) for t in range(PACK)]
         for t in range(PACK):
-            acc = [bank(f"acc{t}{s}") for s in range(2)]
+            width = BANK // 2 if t == 0 else BANK
+            acc = [bank(f"acc{t}{s}", (s if t == 0 else 2 + 2 * t + s) % 8) for s in range(S // width)]
             for z in range(PASSES):
-                for s in range(2):
-                    cols = slice(BANK * s, BANK * (s + 1))
+                for s in range(S // width):
+                    cols = slice(width * s, width * (s + 1))
                     nc.tensor.matmul_mx(
-                        out=acc[s][:],
+                        out=acc[s][:, 0:width],
                         lhsT=wq[z][:, P * t : P * (t + 1)].bitcast(FP8X4),
                         lhsT_scale=wsc[z][:, P * t : P * (t + 1)],
-                        rhs=xw[z][:, cols].bitcast(FP8X4),
+                        rhs=x_codes(z, width * s, width * (s + 1)).bitcast(FP8X4),
                         rhs_scale=xs[4 * z : P, cols],
                         start=(z == 0),
                         stop=(z == PASSES - 1),
                     )
-            nc.scalar.copy(out=h[t][:, 0:BANK], in_=acc[0][:])
-            if t == 0:
-                nc.vector.tensor_copy(out=h[t][:, BANK:S], in_=acc[1][:])
-            else:
-                nc.scalar.copy(out=h[t][:, BANK:S], in_=acc[1][:])
+            for s in range(S // width):
+                cols = slice(width * s, width * (s + 1))
+                if t == 0 and s % 2 == 0:
+                    nc.vector.tensor_copy(out=h[t][:, cols], in_=acc[s][:, 0:width])
+                else:
+                    nc.scalar.copy(out=h[t][:, cols], in_=acc[s][:, 0:width])
 
         n_chunks = V // CHUNK
         g = []
 
         def open_chunk(c):
-            g.append([keep.tile([P, PACK, CHUNK], F32, name=f"g{c}{d}", tag=f"g{d}") for d in range(3)])
+            g.append([keep.tile([P, PACK, CHUNK], F32, name=f"g{c}{d}", tag=f"g{(3 * c + d) % 4}") for d in range(3)])
 
         gb = [[keep.tile([P, CHUNK * PACK], BF16, name=f"gb{c}{d}", align_bytes=64) for d in range(3)] for c in range(n_chunks)]
         z1 = [keep.tile([P, CHUNK * PACK], BF16, name=f"z1{c}", align_bytes=64) for c in range(n_chunks)]
+
+        def gather_order(c):
+            if c == 0:
+                return [(d, t) for t in range(PACK) for d in range(3)]
+            return [(d, t) for d in range(3) for t in range(PACK)]
 
         def gather(c, d, t):
             cols = slice(c * CHUNK // 16, (c + 1) * CHUNK // 16)
@@ -161,19 +176,19 @@ def tile_picked_pna_none_p_kernel(
             )
 
         def mean(c):
-            totals = [bank(f"total{c}{s}") for s in range(CHUNK // SUB)]
-            for t in range(PACK):
-                for d in range(3):
-                    for s, total in enumerate(totals):
-                        nc.tensor.matmul(
-                            total[:, P * t : P * (t + 1)],
-                            lhsT=g[c][d][:, t, SUB * s : SUB * (s + 1)],
-                            rhs=ident[:],
-                            is_transpose=True,
-                            start=(d == 0),
-                            stop=(d == 2),
-                        )
-            back = bank(f"back{c}")
+            totals = [bank(f"total{c}{s}", 2 + 3 * c + s) for s in range(CHUNK // SUB)]
+            order = gather_order(c)
+            for d, t in order:
+                for s, total in enumerate(totals):
+                    nc.tensor.matmul(
+                        total[:, P * t : P * (t + 1)],
+                        lhsT=g[c][d][:, t, SUB * s : SUB * (s + 1)],
+                        rhs=ident_gate[:] if (c, d, t) == (0, 0, PACK - 1) else ident[:],
+                        is_transpose=True,
+                        start=((d, t) == order[0]),
+                        stop=((d, t) == order[-1]),
+                    )
+            back = bank(f"back{c}", 4 + 3 * c)
             for s, total in enumerate(totals):
                 turned = keep.tile([P, H], BF16, name=f"turned{c}{s}", align_bytes=64)
                 nc.scalar.activation(
@@ -191,8 +206,8 @@ def tile_picked_pna_none_p_kernel(
             )
 
         def finish(c):
-            hi = keep.tile([P, CHUNK * PACK], BF16, name=f"hi{c}", align_bytes=64)
-            lo = keep.tile([P, CHUNK * PACK], BF16, name=f"lo{c}", align_bytes=64)
+            hi = keep.tile([P, CHUNK * PACK], BF16, name=f"hi{c}", tag="h2" if c == 0 else "hi", align_bytes=64)
+            lo = keep.tile([P, CHUNK * PACK], BF16, name=f"lo{c}", tag="h3" if c == 0 else "lo", align_bytes=64)
             z2 = keep.tile([P, CHUNK * PACK], BF16, name=f"z2{c}", align_bytes=64)
             z3 = keep.tile([P, CHUNK * PACK], BF16, name=f"z3{c}", align_bytes=64)
             a, b, e = gb[c]
@@ -202,28 +217,46 @@ def tile_picked_pna_none_p_kernel(
             nc.vector.tensor_tensor(out=z3[:], in0=lo[:], in1=e[:], op=MIN)
             zq = [keep.tile([P, CHUNK], U32, name=f"zq{c}{d}", align_bytes=64) for d in range(3)]
             zs = [keep.tile([P, CHUNK], U8, name=f"zs{c}{d}", align_bytes=64) for d in range(3)]
-            for d, z in enumerate((z1[c], z2, z3)):
+            for d, z in ((1, z2), (2, z3)):
                 nc.vector.quantize_mx(out=zq[d][:].bitcast(FP8X4), scales=zs[d][:], in_=z[:])
-            result = keep.tile([P, CHUNK], F32, name=f"result{c}")
-            res = [bank(f"res{c}{s}") for s in range(CHUNK // SUB)]
-            for d in range(3):
-                for s in range(CHUNK // SUB):
-                    cols = slice(SUB * s, SUB * (s + 1))
-                    nc.tensor.matmul_mx(
-                        out=res[s][:, 0:SUB],
-                        lhsT=ww2[d][:].bitcast(FP4X4),
-                        lhsT_scale=ws2[:, d * N : (d + 1) * N],
-                        rhs=zq[d][:, cols].bitcast(FP8X4),
-                        rhs_scale=zs[d][:, cols],
-                        start=(d == 0),
-                        stop=(d == 2),
-                    )
-            if c == n_chunks - 1:
-                nc.vector.tensor_copy(out=result[:, 0:SUB], in_=res[0][:, 0:SUB])
+            last = c == n_chunks - 1
+            step = SUB if last else CHUNK
+            for v0 in range(0, CHUNK, step):
+                cols = slice(v0, v0 + step)
+                nc.vector.quantize_mx(
+                    out=zq[0][:, cols].bitcast(FP8X4), scales=zs[0][:, cols], in_=z1[c][:, PACK * v0 : PACK * (v0 + step)]
+                )
+            if last:
+                res = [bank(f"res{c}{s}", s)[:, 0:SUB] for s in range(CHUNK // SUB)]
+                order = [(d, s) for d in (1, 2, 0) for s in range(CHUNK // SUB)]
             else:
-                nc.scalar.copy(out=result[:, 0:SUB], in_=res[0][:, 0:SUB])
-            nc.scalar.copy(out=result[:, SUB:CHUNK], in_=res[1][:, 0:SUB])
-            nc.sync.dma_start(out=out[:, c * CHUNK : (c + 1) * CHUNK], in_=result[:])
+                shared = bank(f"res{c}", 6)
+                res = [shared[:, SUB * s : SUB * (s + 1)] for s in range(CHUNK // SUB)]
+                order = [(d, s) for s in range(CHUNK // SUB) for d in (1, 2, 0)]
+            for d, s in order:
+                cols = slice(SUB * s, SUB * (s + 1))
+                nc.tensor.matmul_mx(
+                    out=res[s],
+                    lhsT=ww2[d][:].bitcast(FP4X4),
+                    lhsT_scale=ws2[:, d * N : (d + 1) * N],
+                    rhs=zq[d][:, cols].bitcast(FP8X4),
+                    rhs_scale=zs[d][:, cols],
+                    start=(d == 1),
+                    stop=(d == 0),
+                )
+            if last:
+                for s in range(CHUNK // SUB):
+                    result = keep.tile([P, SUB], F32, name=f"result{c}{s}")
+                    if s == 0:
+                        nc.scalar.copy(out=result[:], in_=res[s])
+                    else:
+                        nc.vector.tensor_copy(out=result[:], in_=res[s])
+                    v0 = c * CHUNK + s * SUB
+                    nc.sync.dma_start(out=out[:, v0 : v0 + SUB], in_=result[:])
+            else:
+                result = keep.tile([P, CHUNK], F32, name=f"result{c}")
+                nc.scalar.copy(out=result[:], in_=shared[:, 0:CHUNK])
+                nc.sync.dma_start(out=out[:, c * CHUNK : (c + 1) * CHUNK], in_=result[:])
 
         open_chunk(0)
         for t in range(PACK):

@@ -24,6 +24,7 @@ PASSES = K // (P * PACK)
 BANK = 512
 CHUNK = 256
 SUB = 128
+W_SPLIT = 48
 
 
 def tile_picked_pna_none_p_kernel(
@@ -51,18 +52,19 @@ def tile_picked_pna_none_p_kernel(
         w_raw0 = keep.tile([P, PACK, H], F32, name="w_raw0")
         w_raw1 = [keep.tile([P, PACK, H // 2], F32, name=f"w_raw1{i}") for i in range(2)]
 
-        def load_x(z):
-            nc.sync.dma_start(out=xw_all[z][:], in_=x_words[z].rearrange("p n t -> p (n t)").bitcast(I32))
+        def load_x(z, c0, c1):
+            nc.sync.dma_start(out=xw_all[z][:, c0:c1], in_=x_words[z].rearrange("p n t -> p (n t)").bitcast(I32)[:, c0:c1])
 
-        load_x(0)
+        load_x(0, 0, T // 4)
         nc.sync.dma_start(offs_sb[:], offs)
         for q in range(4):
             nc.sync.dma_start(
                 out=xs_all[32 * q : 32 * q + 8, :].bitcast(I32),
                 in_=x_scales[:, 4 * q : 4 * q + 4, :].bitcast(I32),
             )
+        load_x(0, T // 4, T)
         nc.sync.dma_start(out=w_raw0[:], in_=w_rows[0])
-        load_x(1)
+        load_x(1, 0, T)
         for i in range(2):
             nc.sync.dma_start(out=w_raw1[i][:], in_=w_rows[1][:, :, 256 * i : 256 * (i + 1)])
         for d, pos in enumerate((pos1, pos2, pos3)):
@@ -79,8 +81,6 @@ def tile_picked_pna_none_p_kernel(
 
         ident = keep.tile([P, P], F32, name="ident")
         make_identity(nc, ident[:])
-        ident_gate = keep.tile([P, P], F32, name="ident_gate", tag="g3")
-        make_identity(nc, ident_gate[:])
 
         xw = [keep.tile([P, S], U32, name="xw0", align_bytes=64)]
         xs = keep.tile([P, S], U8, name="xs", align_bytes=64)
@@ -89,137 +89,170 @@ def tile_picked_pna_none_p_kernel(
         wsc = [keep.tile([P, H], U8, name=f"wsc{z}", align_bytes=64) for z in range(PASSES)]
 
         def w_views(z, u, raw, m0, m1):
+            r0 = m0 if z == 0 else 0
             return (
                 w_bf[z][u][:, :, m0:m1, :].rearrange("p e m j -> p m j e"),
-                raw[:].rearrange("p j (m t) -> p m j t", t=PACK)[:, :, :, 2 * u : 2 * u + 2],
+                raw[:].rearrange("p j (m t) -> p m j t", t=PACK)[:, r0 : r0 + m1 - m0, :, 2 * u : 2 * u + 2],
             )
 
         def round_w_scalar(*args):
             dst, src = w_views(*args)
             nc.scalar.activation(out=dst, in_=src, func=COPY)
 
+        def round_w_vector(*args):
+            dst, src = w_views(*args)
+            nc.vector.tensor_copy(out=dst, in_=src)
+
+        def w_scales(z, t0, t1):
+            if z == 0:
+                return wsc[z][:, P * t0 : P * t1]
+            if t0 >= 2:
+                return wsc[z][4:P, P * (t0 - 2) : P * (t1 - 2)]
+            return wsc[z][:, 2 * P * t0 : 2 * P * t0 + P]
+
         def quantize_w(z, t0, t1):
             flat = w_bf[z][t0 // 2][:, t0 % 2 : t0 % 2 + t1 - t0, :, :].rearrange("p e m j -> p (e m j)")
             cols = slice(P * t0, P * t1)
-            nc.vector.quantize_mx(out=wq[z][:, cols].bitcast(FP8X4), scales=wsc[z][:, cols], in_=flat)
+            nc.vector.quantize_mx(out=wq[z][:, cols].bitcast(FP8X4), scales=w_scales(z, t0, t1), in_=flat)
 
-        nc.vector.tensor_copy(out=xw[0][:], in_=xw_all[0][:].bitcast(U32).indirect(offs_sb[:]))
         nc.vector.tensor_copy(out=xs[:], in_=xs_all[:].indirect(offs_sb[:]))
+        nc.vector.tensor_copy(out=xw[0][:], in_=xw_all[0][:].bitcast(U32).indirect(offs_sb[:]))
         round_w_scalar(0, 0, w_raw0, 0, P)
-        round_w_scalar(0, 1, w_raw0, 0, P)
+        round_w_scalar(0, 1, w_raw0, 0, W_SPLIT)
+        round_w_vector(0, 1, w_raw0, W_SPLIT, P)
         quantize_w(0, 0, 2)
-        xw1 = []
-        for i in range(2):
-            if i == 1:
-                quantize_w(0, 2, 4)
-            xw1.append(keep.tile([P, BANK], U32, name=f"xw1{i}", tag=f"w_bf0{i}", align_bytes=64))
-            nc.vector.tensor_copy(out=xw1[i][:], in_=xw_all[1][:].bitcast(U32).indirect(offs_sb[:, 32 * i : 32 * (i + 1)]))
-
-        def x_codes(z, c0, c1):
-            if z == 0:
-                return xw[0][:, c0:c1]
-            return xw1[c0 // BANK][:, c0 % BANK : c0 % BANK + c1 - c0]
-
+        quantize_w(0, 2, 4)
+        xw.append(keep.tile([P, S], U32, name="xw1", tag="w_bf01", align_bytes=64))
+        nc.vector.tensor_copy(out=xw[1][:], in_=xw_all[1][:].bitcast(U32).indirect(offs_sb[:]))
         round_w_scalar(1, 0, w_raw1[0], 0, P // 2)
         round_w_scalar(1, 1, w_raw1[0], 0, P // 2)
         round_w_scalar(1, 0, w_raw1[1], P // 2, P)
         round_w_scalar(1, 1, w_raw1[1], P // 2, P)
         quantize_w(1, 0, 1)
         quantize_w(1, 1, 2)
+
+        h_first = keep.tile([P, S], F32, name="h_first", align_bytes=64)
+        h_rest = keep.tile([P, PACK - 1, S], F32, name="h_rest", align_bytes=64)
+
+        def h_pass(acc, t, z, c0, c1):
+            nc.tensor.matmul_mx(
+                out=acc,
+                lhsT=wq[z][:, P * t : P * (t + 1)].bitcast(FP8X4),
+                lhsT_scale=w_scales(z, t, t + 1),
+                rhs=xw[z][:, c0:c1].bitcast(FP8X4),
+                rhs_scale=xs[4 * z : P, c0:c1],
+                start=(z == 0),
+                stop=(z == PASSES - 1),
+            )
+
+        quarter = S // 4
+        acc = [bank(f"acc0{s}", s) for s in range(4)]
+        for z in range(PASSES):
+            for s in range(4):
+                h_pass(acc[s][:, 0:quarter], 0, z, quarter * s, quarter * (s + 1))
+        for s in range(4):
+            cols = slice(quarter * s, quarter * (s + 1))
+            if s % 2 == 0:
+                nc.vector.tensor_copy(out=h_first[:, cols], in_=acc[s][:, 0:quarter])
+            else:
+                nc.scalar.copy(out=h_first[:, cols], in_=acc[s][:, 0:quarter])
         quantize_w(1, 2, 4)
 
-        h = [keep.tile([P, S], F32, name=f"h{t}", tag=f"h{t}", align_bytes=64) for t in range(PACK)]
-        for t in range(PACK):
-            width = BANK // 2 if t == 0 else BANK
-            acc = [bank(f"acc{t}{s}", (s if t == 0 else 2 + 2 * t + s) % 8) for s in range(S // width)]
+        edge = S - SUB
+        for t in range(1, PACK):
+            wide = bank(f"acc{t}a", (2 + 2 * t) % 8)
+            narrow = bank(f"acc{t}b", (3 + 2 * t) % 8)
             for z in range(PASSES):
-                for s in range(S // width):
-                    cols = slice(width * s, width * (s + 1))
-                    nc.tensor.matmul_mx(
-                        out=acc[s][:, 0:width],
-                        lhsT=wq[z][:, P * t : P * (t + 1)].bitcast(FP8X4),
-                        lhsT_scale=wsc[z][:, P * t : P * (t + 1)],
-                        rhs=x_codes(z, width * s, width * (s + 1)).bitcast(FP8X4),
-                        rhs_scale=xs[4 * z : P, cols],
-                        start=(z == 0),
-                        stop=(z == PASSES - 1),
+                h_pass(wide[:], t, z, 0, BANK)
+                h_pass(narrow[:, 0:quarter], t, z, BANK, BANK + quarter)
+            for z in range(PASSES):
+                h_pass(narrow[:, quarter : quarter + SUB], t, z, BANK + quarter, edge)
+            nc.scalar.copy(out=h_rest[:, t - 1, 0:BANK], in_=wide[:])
+            nc.scalar.copy(out=h_rest[:, t - 1, BANK:edge], in_=narrow[:, 0 : edge - BANK])
+        joint = bank("joint", 7)
+        for t in range(1, PACK):
+            for z in range(PASSES):
+                h_pass(joint[:, SUB * (t - 1) : SUB * t], t, z, edge, S)
+        nc.scalar.copy(out=h_rest[:, :, edge:S], in_=joint[:, 0 : 3 * SUB].rearrange("p (t c) -> p t c", c=SUB))
+
+        halves = V // CHUNK
+        g = [keep.tile([P, PACK, V], F32, name=f"g{d}", align_bytes=64) for d in range(3)]
+        gb = [keep.tile([P, V * PACK], BF16, name=f"gb{d}", align_bytes=64) for d in range(3)]
+        order = [(d, 0) for d in range(3)] + [(d, t) for d in range(3) for t in range(1, PACK)]
+        totals = [[bank(f"total{u}{c}", ((0, 1), (7, 2))[u][c]) for c in range(halves)] for u in range(2)]
+        for d, t in order:
+            window = h_first[:] if t == 0 else h_rest[:, t - 1, :]
+            nc.vector.tensor_copy(out=g[d][:, t, :], in_=window.indirect(pos_sb[d][:]))
+        order.remove((2, 1))
+        order.insert(order.index((1, 1)) + 1, (2, 1))
+        for d, t in order:
+            for c in range(halves):
+                for s in range(2):
+                    v0 = CHUNK * c + SUB * s
+                    col = P * (2 * s + t % 2)
+                    nc.tensor.matmul(
+                        totals[t // 2][c][:, col : col + P],
+                        lhsT=g[d][:, t, v0 : v0 + SUB],
+                        rhs=ident[:],
+                        is_transpose=True,
+                        start=(d == 0 and t % 2 == 0 and s == 0),
+                        stop=(d == 2 and t % 2 == 1 and s == 1),
                     )
-            for s in range(S // width):
-                cols = slice(width * s, width * (s + 1))
-                if t == 0 and s % 2 == 0:
-                    nc.vector.tensor_copy(out=h[t][:, cols], in_=acc[s][:, 0:width])
-                else:
-                    nc.scalar.copy(out=h[t][:, cols], in_=acc[s][:, 0:width])
 
-        n_chunks = V // CHUNK
-        g = []
-
-        def open_chunk(c):
-            g.append([keep.tile([P, PACK, CHUNK], F32, name=f"g{c}{d}", tag=f"g{(3 * c + d) % 4}") for d in range(3)])
-
-        gb = [[keep.tile([P, CHUNK * PACK], BF16, name=f"gb{c}{d}", align_bytes=64) for d in range(3)] for c in range(n_chunks)]
-        z1 = [keep.tile([P, CHUNK * PACK], BF16, name=f"z1{c}", align_bytes=64) for c in range(n_chunks)]
-
-        def gather_order(c):
-            if c == 0:
-                return [(d, t) for t in range(PACK) for d in range(3)]
-            return [(d, t) for d in range(3) for t in range(PACK)]
-
-        def gather(c, d, t):
-            cols = slice(c * CHUNK // 16, (c + 1) * CHUNK // 16)
-            nc.vector.tensor_copy(out=g[c][d][:, t, :], in_=h[t][:].indirect(pos_sb[d][:, cols]))
-
-        def cast(c, d):
+        def cast(d, v0, v1):
             nc.scalar.copy(
-                out=gb[c][d][:].rearrange("p (v i t) -> p v t i", i=4, t=PACK),
-                in_=g[c][d][:].rearrange("p t (v i) -> p v t i", i=4),
+                out=gb[d][:, PACK * v0 : PACK * v1].rearrange("p (v i t) -> p v t i", i=4, t=PACK),
+                in_=g[d][:, :, v0:v1].rearrange("p t (v i) -> p v t i", i=4),
             )
 
-        def mean(c):
-            totals = [bank(f"total{c}{s}", 2 + 3 * c + s) for s in range(CHUNK // SUB)]
-            order = gather_order(c)
-            for d, t in order:
-                for s, total in enumerate(totals):
-                    nc.tensor.matmul(
-                        total[:, P * t : P * (t + 1)],
-                        lhsT=g[c][d][:, t, SUB * s : SUB * (s + 1)],
-                        rhs=ident_gate[:] if (c, d, t) == (0, 0, PACK - 1) else ident[:],
-                        is_transpose=True,
-                        start=((d, t) == order[0]),
-                        stop=((d, t) == order[-1]),
-                    )
-            back = bank(f"back{c}", 4 + 3 * c)
-            for s, total in enumerate(totals):
-                turned = keep.tile([P, H], BF16, name=f"turned{c}{s}", align_bytes=64)
-                nc.scalar.activation(
-                    out=turned[:].rearrange("v (u p e) -> v u p e", u=2, e=2),
-                    in_=total[:].rearrange("v (u e p) -> v u p e", u=2, e=2),
-                    func=COPY,
-                    scale=1.0 / 3.0,
-                )
-                pairs = turned[:].bitcast(F32)
-                for u in range(2):
-                    nc.tensor.transpose(back[:, P * (2 * s + u) : P * (2 * s + u + 1)], pairs[:, P * u : P * (u + 1)], ident[:])
+        back = [bank(f"back{c}", 4 + c) for c in range(halves)]
+        z1 = [keep.tile([P, CHUNK * PACK], BF16, name=f"z1{c}", align_bytes=64) for c in range(halves)]
+
+        def turn(u, c):
+            turned = keep.tile([P, 2 * P * 2], BF16, name=f"turned{u}{c}", align_bytes=64)
+            nc.scalar.activation(
+                out=turned[:].rearrange("v (s p e) -> v s p e", s=2, e=2),
+                in_=totals[u][c][:].rearrange("v (s e p) -> v s p e", s=2, e=2),
+                func=COPY,
+                scale=1.0 / 3.0,
+            )
+            pairs = turned[:].bitcast(F32)
+            for s in range(2):
+                nc.tensor.transpose(back[c][:, P * (2 * s + u) : P * (2 * s + u + 1)], pairs[:, P * s : P * (s + 1)], ident[:])
+
+        def weave(c):
             nc.scalar.copy(
                 out=z1[c][:].bitcast(F32).rearrange("p (s v u) -> p s v u", s=2, u=2),
-                in_=back[:].rearrange("p (s u v) -> p s v u", s=2, u=2),
+                in_=back[c][:].rearrange("p (s u v) -> p s v u", s=2, u=2),
             )
 
+        cast(0, 0, V)
+        cast(1, 0, V)
+        turn(0, 0)
+        turn(0, 1)
+        cast(2, 0, CHUNK)
+        turn(1, 0)
+        cast(2, CHUNK, V)
+        weave(0)
+        turn(1, 1)
+        weave(1)
+
+        hi = keep.tile([P, V * PACK], BF16, name="hi", align_bytes=64)
+        lo = keep.tile([P, V * PACK], BF16, name="lo", align_bytes=64)
+        nc.vector.tensor_tensor(out=hi[:], in0=gb[0][:], in1=gb[1][:], op=MAX)
+        nc.vector.tensor_tensor(out=lo[:], in0=gb[0][:], in1=gb[1][:], op=MIN)
+
         def finish(c):
-            hi = keep.tile([P, CHUNK * PACK], BF16, name=f"hi{c}", tag="h2" if c == 0 else "hi", align_bytes=64)
-            lo = keep.tile([P, CHUNK * PACK], BF16, name=f"lo{c}", tag="h3" if c == 0 else "lo", align_bytes=64)
             z2 = keep.tile([P, CHUNK * PACK], BF16, name=f"z2{c}", align_bytes=64)
             z3 = keep.tile([P, CHUNK * PACK], BF16, name=f"z3{c}", align_bytes=64)
-            a, b, e = gb[c]
-            nc.vector.tensor_tensor(out=hi[:], in0=a[:], in1=b[:], op=MAX)
-            nc.vector.tensor_tensor(out=lo[:], in0=a[:], in1=b[:], op=MIN)
-            nc.vector.tensor_tensor(out=z2[:], in0=hi[:], in1=e[:], op=MAX)
-            nc.vector.tensor_tensor(out=z3[:], in0=lo[:], in1=e[:], op=MIN)
+            part = slice(CHUNK * PACK * c, CHUNK * PACK * (c + 1))
+            nc.vector.tensor_tensor(out=z2[:], in0=hi[:, part], in1=gb[2][:, part], op=MAX)
+            nc.vector.tensor_tensor(out=z3[:], in0=lo[:, part], in1=gb[2][:, part], op=MIN)
             zq = [keep.tile([P, CHUNK], U32, name=f"zq{c}{d}", align_bytes=64) for d in range(3)]
             zs = [keep.tile([P, CHUNK], U8, name=f"zs{c}{d}", align_bytes=64) for d in range(3)]
             for d, z in ((1, z2), (2, z3)):
                 nc.vector.quantize_mx(out=zq[d][:].bitcast(FP8X4), scales=zs[d][:], in_=z[:])
-            last = c == n_chunks - 1
+            last = c == halves - 1
             step = SUB if last else CHUNK
             for v0 in range(0, CHUNK, step):
                 cols = slice(v0, v0 + step)
@@ -227,10 +260,10 @@ def tile_picked_pna_none_p_kernel(
                     out=zq[0][:, cols].bitcast(FP8X4), scales=zs[0][:, cols], in_=z1[c][:, PACK * v0 : PACK * (v0 + step)]
                 )
             if last:
-                res = [bank(f"res{c}{s}", s)[:, 0:SUB] for s in range(CHUNK // SUB)]
+                res = [bank(f"res{c}{s}", (6, 0)[s])[:, 0:SUB] for s in range(CHUNK // SUB)]
                 order = [(d, s) for d in (1, 2, 0) for s in range(CHUNK // SUB)]
             else:
-                shared = bank(f"res{c}", 6)
+                shared = bank(f"res{c}", 3)
                 res = [shared[:, SUB * s : SUB * (s + 1)] for s in range(CHUNK // SUB)]
                 order = [(d, s) for s in range(CHUNK // SUB) for d in (1, 2, 0)]
             for d, s in order:
@@ -258,18 +291,5 @@ def tile_picked_pna_none_p_kernel(
                 nc.scalar.copy(out=result[:], in_=shared[:, 0:CHUNK])
                 nc.sync.dma_start(out=out[:, c * CHUNK : (c + 1) * CHUNK], in_=result[:])
 
-        open_chunk(0)
-        for t in range(PACK):
-            for d in range(3):
-                gather(0, d, t)
-        for d in range(3):
-            cast(0, d)
-        mean(0)
-        open_chunk(1)
-        for d in range(3):
-            for t in range(PACK):
-                gather(1, d, t)
-            cast(1, d)
-        mean(1)
         finish(0)
         finish(1)

@@ -15,6 +15,9 @@ U8 = mybir.dt.uint8
 FP8X4 = mybir.dt.float8_e4m3fn_x4
 FP4X4 = mybir.dt.float4_e2m1fn_x4
 COPY = mybir.ActivationFunctionType.Copy
+RELU = mybir.ActivationFunctionType.Relu
+ADD = mybir.AluOpType.add
+SUBTRACT = mybir.AluOpType.subtract
 MAX = mybir.AluOpType.max
 MIN = mybir.AluOpType.min
 
@@ -132,7 +135,8 @@ def tile_picked_pna_none_p_kernel(
         quantize_w(1, 1, 2)
 
         h_first = keep.tile([P, S], F32, name="h_first", align_bytes=64)
-        h_rest = keep.tile([P, PACK - 1, S], F32, name="h_rest", align_bytes=64)
+        h_second = keep.tile([P, S], F32, name="h_second", align_bytes=64)
+        h_rest = keep.tile([P, 2, S], F32, name="h_rest", align_bytes=64)
 
         def h_pass(acc, t, z, c0, c1):
             nc.tensor.matmul_mx(
@@ -158,55 +162,73 @@ def tile_picked_pna_none_p_kernel(
                 nc.scalar.copy(out=h_first[:, cols], in_=acc[s][:, 0:quarter])
         quantize_w(1, 2, 4)
 
-        edge = S - SUB
-        for t in range(1, PACK):
-            wide = bank(f"acc{t}a", (2 + 2 * t) % 8)
-            narrow = bank(f"acc{t}b", (3 + 2 * t) % 8)
-            for z in range(PASSES):
-                h_pass(wide[:], t, z, 0, BANK)
-                h_pass(narrow[:, 0:quarter], t, z, BANK, BANK + quarter)
-            for z in range(PASSES):
-                h_pass(narrow[:, quarter : quarter + SUB], t, z, BANK + quarter, edge)
-            nc.scalar.copy(out=h_rest[:, t - 1, 0:BANK], in_=wide[:])
-            nc.scalar.copy(out=h_rest[:, t - 1, BANK:edge], in_=narrow[:, 0 : edge - BANK])
-        joint = bank("joint", 7)
-        for t in range(1, PACK):
-            for z in range(PASSES):
-                h_pass(joint[:, SUB * (t - 1) : SUB * t], t, z, edge, S)
-        nc.scalar.copy(out=h_rest[:, :, edge:S], in_=joint[:, 0 : 3 * SUB].rearrange("p (t c) -> p t c", c=SUB))
+        def pair_pass(acc, z, c0, first, last):
+            for e in range(2):
+                t = 2 + e
+                nc.tensor.matmul_mx(
+                    out=acc[:, quarter * e : quarter * (e + 1)],
+                    lhsT=wq[z][:, P * t : P * (t + 1)].bitcast(FP8X4),
+                    lhsT_scale=w_scales(z, t, t + 1),
+                    rhs=xw[z][:, c0 : c0 + quarter].bitcast(FP8X4),
+                    rhs_scale=xs[4 * z : P, c0 : c0 + quarter],
+                    start=(first and e == 0),
+                    stop=(last and e == 1),
+                )
+
+        acc1 = [bank(f"acc1{s}", 4 + s) for s in range(2)]
+        for z in range(PASSES):
+            for s in range(2):
+                h_pass(acc1[s][:], 1, z, BANK * s, BANK * (s + 1))
+        for s in range(2):
+            nc.scalar.copy(out=h_second[:, BANK * s : BANK * (s + 1)], in_=acc1[s][:])
+        wide2, both_a, wide3, both_b = bank("wide2", 6), bank("both_a", 7), bank("wide3", 0), bank("both_b", 1)
+        for z in range(PASSES):
+            h_pass(wide2[:], 2, z, 0, BANK)
+            pair_pass(both_a, z, BANK, z == 0, z == PASSES - 1)
+        for z in range(PASSES):
+            h_pass(wide3[:], 3, z, 0, BANK)
+        for z in range(PASSES):
+            pair_pass(both_b, z, BANK + quarter, z == 0, z == PASSES - 1)
+        nc.scalar.copy(out=h_rest[:, 0, 0:BANK], in_=wide2[:])
+        nc.scalar.copy(out=h_rest[:, :, BANK : BANK + quarter], in_=both_a[:].rearrange("p (e c) -> p e c", e=2))
+        nc.scalar.copy(out=h_rest[:, 1, 0:BANK], in_=wide3[:])
+        nc.scalar.copy(out=h_rest[:, :, BANK + quarter : S], in_=both_b[:].rearrange("p (e c) -> p e c", e=2))
 
         halves = V // CHUNK
-        g = [keep.tile([P, PACK, V], F32, name=f"g{d}", align_bytes=64) for d in range(3)]
-        gb = [keep.tile([P, V * PACK], BF16, name=f"gb{d}", align_bytes=64) for d in range(3)]
-        order = [(d, 0) for d in range(3)] + [(d, t) for d in range(3) for t in range(1, PACK)]
-        totals = [[bank(f"total{u}{c}", ((0, 1), (7, 2))[u][c]) for c in range(halves)] for u in range(2)]
-        for d, t in order:
-            window = h_first[:] if t == 0 else h_rest[:, t - 1, :]
-            nc.vector.tensor_copy(out=g[d][:, t, :], in_=window.indirect(pos_sb[d][:]))
-        order.remove((2, 1))
-        order.insert(order.index((1, 1)) + 1, (2, 1))
-        for d, t in order:
+        g = [[keep.tile([P, 2, V], F32, name=f"g{d}{u}", align_bytes=64) for u in range(2)] for d in range(3)]
+        gb = [keep.tile([P, V * 2], BF16, name=f"gb{d}", align_bytes=64) for d in range(2)]
+        third = [keep.tile([P, 2, CHUNK * 2], BF16, name=f"third{c}", align_bytes=64) for c in range(halves)]
+        hi = keep.tile([P, 2, V * 2], BF16, name="hi", align_bytes=64)
+        lo = keep.tile([P, 2, V * 2], BF16, name="lo", align_bytes=64)
+        totals = [[bank(f"total{u}{c}", 2 + 2 * u + c) for c in range(halves)] for u in range(2)]
+        back = [bank(f"back{c}", 6 + c) for c in range(halves)]
+        z1 = [keep.tile([P, CHUNK * PACK], BF16, name=f"z1{c}", align_bytes=64) for c in range(halves)]
+        windows = [h_first[:], h_second[:], h_rest[:, 0, :], h_rest[:, 1, :]]
+
+        def gather(d, t):
+            u, e = divmod(t, 2)
+            nc.vector.tensor_copy(out=g[d][u][:, e, :], in_=windows[t].indirect(pos_sb[d][:]))
+
+        def add_up(d, t, first, last):
+            u, e = divmod(t, 2)
             for c in range(halves):
                 for s in range(2):
                     v0 = CHUNK * c + SUB * s
-                    col = P * (2 * s + t % 2)
+                    col = P * (2 * s + e)
                     nc.tensor.matmul(
-                        totals[t // 2][c][:, col : col + P],
-                        lhsT=g[d][:, t, v0 : v0 + SUB],
+                        totals[u][c][:, col : col + P],
+                        lhsT=g[d][u][:, e, v0 : v0 + SUB],
                         rhs=ident[:],
                         is_transpose=True,
-                        start=(d == 0 and t % 2 == 0 and s == 0),
-                        stop=(d == 2 and t % 2 == 1 and s == 1),
+                        start=(first and s == 0),
+                        stop=(last and s == 1),
                     )
 
-        def cast(d, v0, v1):
+        def cast(dst, d, u, v0, v1):
             nc.scalar.copy(
-                out=gb[d][:, PACK * v0 : PACK * v1].rearrange("p (v i t) -> p v t i", i=4, t=PACK),
-                in_=g[d][:, :, v0:v1].rearrange("p t (v i) -> p v t i", i=4),
+                out=dst.rearrange("p (v i e) -> p v e i", i=4, e=2),
+                in_=g[d][u][:, :, v0:v1].rearrange("p e (v i) -> p v e i", i=4),
             )
-
-        back = [bank(f"back{c}", 4 + c) for c in range(halves)]
-        z1 = [keep.tile([P, CHUNK * PACK], BF16, name=f"z1{c}", align_bytes=64) for c in range(halves)]
 
         def turn(u, c):
             turned = keep.tile([P, 2 * P * 2], BF16, name=f"turned{u}{c}", align_bytes=64)
@@ -226,28 +248,47 @@ def tile_picked_pna_none_p_kernel(
                 in_=back[c][:].rearrange("p (s u v) -> p s v u", s=2, u=2),
             )
 
-        cast(0, 0, V)
-        cast(1, 0, V)
-        turn(0, 0)
-        turn(0, 1)
-        cast(2, 0, CHUNK)
-        turn(1, 0)
-        cast(2, CHUNK, V)
-        weave(0)
-        turn(1, 1)
-        weave(1)
+        def compare_by_difference(e):
+            a, b = g[0][0][:, e, :], g[1][0][:, e, :]
+            diff = keep.tile([P, V], F32, name=f"diff{e}", align_bytes=64)
+            excess = keep.tile([P, V], F32, name=f"excess{e}", align_bytes=64)
+            nc.gpsimd.tensor_tensor(out=diff[:], in0=a, in1=b, op=SUBTRACT)
+            nc.scalar.activation(out=excess[:], in_=diff[:], func=RELU)
+            nc.gpsimd.tensor_tensor(out=hi[:, 0, :].rearrange("p (v e) -> p v e", e=2)[:, :, e], in0=b, in1=excess[:], op=ADD)
+            nc.gpsimd.tensor_tensor(out=lo[:, 0, :].rearrange("p (v e) -> p v e", e=2)[:, :, e], in0=a, in1=excess[:], op=SUBTRACT)
 
-        hi = keep.tile([P, V * PACK], BF16, name="hi", align_bytes=64)
-        lo = keep.tile([P, V * PACK], BF16, name="lo", align_bytes=64)
-        nc.vector.tensor_tensor(out=hi[:], in0=gb[0][:], in1=gb[1][:], op=MAX)
-        nc.vector.tensor_tensor(out=lo[:], in0=gb[0][:], in1=gb[1][:], op=MIN)
+        orders = [[(d, t) for t in (0, 1) for d in range(3)], [(d, t) for d in range(3) for t in (2, 3)]]
+        for u in range(2):
+            for d, t in orders[u]:
+                gather(d, t)
+            for i, (d, t) in enumerate(orders[u]):
+                add_up(d, t, i == 0, i == len(orders[u]) - 1)
+            if u == 0:
+                compare_by_difference(0)
+                compare_by_difference(1)
+            else:
+                cast(gb[0][:], 0, u, 0, V)
+                cast(gb[1][:], 1, u, 0, V)
+            for c in range(halves):
+                cast(third[c][:, u, :], 2, u, CHUNK * c, CHUNK * (c + 1))
+            for c in range(halves):
+                turn(u, c)
+        nc.vector.tensor_tensor(out=hi[:, 1, :], in0=gb[0][:], in1=gb[1][:], op=MAX)
+        nc.vector.tensor_tensor(out=lo[:, 1, :], in0=gb[0][:], in1=gb[1][:], op=MIN)
+        for c in range(halves):
+            weave(c)
+
+        def woven(pairs):
+            return pairs.rearrange("p u (v e) -> p v u e", e=2)
 
         def finish(c):
             z2 = keep.tile([P, CHUNK * PACK], BF16, name=f"z2{c}", align_bytes=64)
             z3 = keep.tile([P, CHUNK * PACK], BF16, name=f"z3{c}", align_bytes=64)
-            part = slice(CHUNK * PACK * c, CHUNK * PACK * (c + 1))
-            nc.vector.tensor_tensor(out=z2[:], in0=hi[:, part], in1=gb[2][:, part], op=MAX)
-            nc.vector.tensor_tensor(out=z3[:], in0=lo[:, part], in1=gb[2][:, part], op=MIN)
+            part = slice(CHUNK * 2 * c, CHUNK * 2 * (c + 1))
+            for z, two, op in ((z2, hi, MAX), (z3, lo, MIN)):
+                nc.vector.tensor_tensor(
+                    out=z[:].rearrange("p (v u e) -> p v u e", u=2, e=2), in0=woven(two[:, :, part]), in1=woven(third[c][:]), op=op
+                )
             zq = [keep.tile([P, CHUNK], U32, name=f"zq{c}{d}", align_bytes=64) for d in range(3)]
             zs = [keep.tile([P, CHUNK], U8, name=f"zs{c}{d}", align_bytes=64) for d in range(3)]
             for d, z in ((1, z2), (2, z3)):
@@ -260,10 +301,10 @@ def tile_picked_pna_none_p_kernel(
                     out=zq[0][:, cols].bitcast(FP8X4), scales=zs[0][:, cols], in_=z1[c][:, PACK * v0 : PACK * (v0 + step)]
                 )
             if last:
-                res = [bank(f"res{c}{s}", (6, 0)[s])[:, 0:SUB] for s in range(CHUNK // SUB)]
+                res = [bank(f"res{c}{s}", (1, 2)[s])[:, 0:SUB] for s in range(CHUNK // SUB)]
                 order = [(d, s) for d in (1, 2, 0) for s in range(CHUNK // SUB)]
             else:
-                shared = bank(f"res{c}", 3)
+                shared = bank(f"res{c}", 0)
                 res = [shared[:, SUB * s : SUB * (s + 1)] for s in range(CHUNK // SUB)]
                 order = [(d, s) for s in range(CHUNK // SUB) for d in (1, 2, 0)]
             for d, s in order:

@@ -27,7 +27,7 @@ PASSES = K // (P * PACK)
 BANK = 512
 CHUNK = 256
 SUB = 128
-W_SPLIT = 48
+X_FIRST = 3 * T // 8
 
 
 def tile_picked_pna_none_p_kernel(
@@ -58,14 +58,14 @@ def tile_picked_pna_none_p_kernel(
         def load_x(z, c0, c1):
             nc.sync.dma_start(out=xw_all[z][:, c0:c1], in_=x_words[z].rearrange("p n t -> p (n t)").bitcast(I32)[:, c0:c1])
 
-        load_x(0, 0, T // 4)
+        load_x(0, 0, X_FIRST)
         nc.sync.dma_start(offs_sb[:], offs)
         for q in range(4):
             nc.sync.dma_start(
                 out=xs_all[32 * q : 32 * q + 8, :].bitcast(I32),
                 in_=x_scales[:, 4 * q : 4 * q + 4, :].bitcast(I32),
             )
-        load_x(0, T // 4, T)
+        load_x(0, X_FIRST, T)
         nc.sync.dma_start(out=w_raw0[:], in_=w_rows[0])
         load_x(1, 0, T)
         for i in range(2):
@@ -102,10 +102,6 @@ def tile_picked_pna_none_p_kernel(
             dst, src = w_views(*args)
             nc.scalar.activation(out=dst, in_=src, func=COPY)
 
-        def round_w_vector(*args):
-            dst, src = w_views(*args)
-            nc.vector.tensor_copy(out=dst, in_=src)
-
         def w_scales(z, t0, t1):
             if z == 0:
                 return wsc[z][:, P * t0 : P * t1]
@@ -121,12 +117,11 @@ def tile_picked_pna_none_p_kernel(
         nc.vector.tensor_copy(out=xs[:], in_=xs_all[:].indirect(offs_sb[:]))
         nc.vector.tensor_copy(out=xw[0][:], in_=xw_all[0][:].bitcast(U32).indirect(offs_sb[:]))
         round_w_scalar(0, 0, w_raw0, 0, P)
-        round_w_scalar(0, 1, w_raw0, 0, W_SPLIT)
-        round_w_vector(0, 1, w_raw0, W_SPLIT, P)
+        round_w_scalar(0, 1, w_raw0, 0, P)
         quantize_w(0, 0, 2)
-        quantize_w(0, 2, 4)
-        xw.append(keep.tile([P, S], U32, name="xw1", tag="w_bf01", align_bytes=64))
+        xw.append(keep.tile([P, S], U32, name="xw1", tag="w_bf00", align_bytes=64))
         nc.vector.tensor_copy(out=xw[1][:], in_=xw_all[1][:].bitcast(U32).indirect(offs_sb[:]))
+        quantize_w(0, 2, 4)
         round_w_scalar(1, 0, w_raw1[0], 0, P // 2)
         round_w_scalar(1, 1, w_raw1[0], 0, P // 2)
         round_w_scalar(1, 0, w_raw1[1], P // 2, P)
@@ -181,7 +176,7 @@ def tile_picked_pna_none_p_kernel(
                 h_pass(acc1[s][:], 1, z, BANK * s, BANK * (s + 1))
         for s in range(2):
             nc.scalar.copy(out=h_second[:, BANK * s : BANK * (s + 1)], in_=acc1[s][:])
-        wide2, both_a, wide3, both_b = bank("wide2", 6), bank("both_a", 7), bank("wide3", 0), bank("both_b", 1)
+        wide2, both_a, wide3, both_b = bank("wide2", 6), bank("both_a", 0), bank("wide3", 1), bank("both_b", 2)
         for z in range(PASSES):
             h_pass(wide2[:], 2, z, 0, BANK)
             pair_pass(both_a, z, BANK, z == 0, z == PASSES - 1)
@@ -200,8 +195,8 @@ def tile_picked_pna_none_p_kernel(
         third = [keep.tile([P, 2, CHUNK * 2], BF16, name=f"third{c}", align_bytes=64) for c in range(halves)]
         hi = keep.tile([P, 2, V * 2], BF16, name="hi", align_bytes=64)
         lo = keep.tile([P, 2, V * 2], BF16, name="lo", align_bytes=64)
-        totals = [[bank(f"total{u}{c}", 2 + 2 * u + c) for c in range(halves)] for u in range(2)]
-        back = [bank(f"back{c}", 6 + c) for c in range(halves)]
+        totals = [[bank(f"total{u}{c}", ((3, 7), (4, 5))[u][c]) for c in range(halves)] for u in range(2)]
+        back = [bank(f"back{c}", (6, 2)[c]) for c in range(halves)]
         z1 = [keep.tile([P, CHUNK * PACK], BF16, name=f"z1{c}", align_bytes=64) for c in range(halves)]
         windows = [h_first[:], h_second[:], h_rest[:, 0, :], h_rest[:, 1, :]]
 
@@ -281,56 +276,58 @@ def tile_picked_pna_none_p_kernel(
         def woven(pairs):
             return pairs.rearrange("p u (v e) -> p v u e", e=2)
 
-        def finish(c):
-            z2 = keep.tile([P, CHUNK * PACK], BF16, name=f"z2{c}", align_bytes=64)
-            z3 = keep.tile([P, CHUNK * PACK], BF16, name=f"z3{c}", align_bytes=64)
-            part = slice(CHUNK * 2 * c, CHUNK * 2 * (c + 1))
-            for z, two, op in ((z2, hi, MAX), (z3, lo, MIN)):
-                nc.vector.tensor_tensor(
-                    out=z[:].rearrange("p (v u e) -> p v u e", u=2, e=2), in0=woven(two[:, :, part]), in1=woven(third[c][:]), op=op
-                )
-            zq = [keep.tile([P, CHUNK], U32, name=f"zq{c}{d}", align_bytes=64) for d in range(3)]
-            zs = [keep.tile([P, CHUNK], U8, name=f"zs{c}{d}", align_bytes=64) for d in range(3)]
-            for d, z in ((1, z2), (2, z3)):
-                nc.vector.quantize_mx(out=zq[d][:].bitcast(FP8X4), scales=zs[d][:], in_=z[:])
-            last = c == halves - 1
-            step = SUB if last else CHUNK
-            for v0 in range(0, CHUNK, step):
-                cols = slice(v0, v0 + step)
-                nc.vector.quantize_mx(
-                    out=zq[0][:, cols].bitcast(FP8X4), scales=zs[0][:, cols], in_=z1[c][:, PACK * v0 : PACK * (v0 + step)]
-                )
-            if last:
-                res = [bank(f"res{c}{s}", (1, 2)[s])[:, 0:SUB] for s in range(CHUNK // SUB)]
-                order = [(d, s) for d in (1, 2, 0) for s in range(CHUNK // SUB)]
-            else:
-                shared = bank(f"res{c}", 0)
-                res = [shared[:, SUB * s : SUB * (s + 1)] for s in range(CHUNK // SUB)]
-                order = [(d, s) for s in range(CHUNK // SUB) for d in (1, 2, 0)]
-            for d, s in order:
-                cols = slice(SUB * s, SUB * (s + 1))
-                nc.tensor.matmul_mx(
-                    out=res[s],
-                    lhsT=ww2[d][:].bitcast(FP4X4),
-                    lhsT_scale=ws2[:, d * N : (d + 1) * N],
-                    rhs=zq[d][:, cols].bitcast(FP8X4),
-                    rhs_scale=zs[d][:, cols],
-                    start=(d == 1),
-                    stop=(d == 0),
-                )
-            if last:
-                for s in range(CHUNK // SUB):
-                    result = keep.tile([P, SUB], F32, name=f"result{c}{s}")
-                    if s == 0:
-                        nc.scalar.copy(out=result[:], in_=res[s])
-                    else:
-                        nc.vector.tensor_copy(out=result[:], in_=res[s])
-                    v0 = c * CHUNK + s * SUB
-                    nc.sync.dma_start(out=out[:, v0 : v0 + SUB], in_=result[:])
-            else:
-                result = keep.tile([P, CHUNK], F32, name=f"result{c}")
-                nc.scalar.copy(out=result[:], in_=shared[:, 0:CHUNK])
-                nc.sync.dma_start(out=out[:, c * CHUNK : (c + 1) * CHUNK], in_=result[:])
+        zq = [[keep.tile([P, CHUNK], U32, name=f"zq{c}{d}", align_bytes=64) for d in range(3)] for c in range(halves)]
+        zs = [[keep.tile([P, CHUNK], U8, name=f"zs{c}{d}", align_bytes=64) for d in range(3)] for c in range(halves)]
+        res = [bank(f"res{i}", (0, 1, 3, 7)[i])[:, 0:SUB] for i in range(V // SUB)]
 
-        finish(0)
-        finish(1)
+        def product(d, c, s):
+            cols = slice(SUB * s, SUB * (s + 1))
+            nc.tensor.matmul_mx(
+                out=res[2 * c + s],
+                lhsT=ww2[d][:].bitcast(FP4X4),
+                lhsT_scale=ws2[:, d * N : (d + 1) * N],
+                rhs=zq[c][d][:, cols].bitcast(FP8X4),
+                rhs_scale=zs[c][d][:, cols],
+                start=(d == 1),
+                stop=(d == 0),
+            )
+
+        z = [[z1[c]] + [keep.tile([P, CHUNK * PACK], BF16, name=f"edge{c}{d}", align_bytes=64) for d in (1, 2)] for c in range(halves)]
+
+        def compare_third(d, c):
+            two, op = ((hi, MAX), (lo, MIN))[d - 1]
+            nc.vector.tensor_tensor(
+                out=z[c][d][:].rearrange("p (v u e) -> p v u e", u=2, e=2),
+                in0=woven(two[:, :, CHUNK * 2 * c : CHUNK * 2 * (c + 1)]),
+                in1=woven(third[c][:]),
+                op=op,
+            )
+
+        def multiply(d, c, v0, v1):
+            nc.vector.quantize_mx(out=zq[c][d][:, v0:v1].bitcast(FP8X4), scales=zs[c][d][:, v0:v1], in_=z[c][d][:, PACK * v0 : PACK * v1])
+            for s in range(v0 // SUB, v1 // SUB):
+                product(d, c, s)
+
+        def store(c, v0, v1):
+            result = keep.tile([P, v1 - v0], F32, name=f"result{c}{v0}")
+            for s in range(v0 // SUB, v1 // SUB):
+                cols = slice(SUB * s - v0, SUB * (s + 1) - v0)
+                if (c, s) == (1, 1):
+                    nc.vector.tensor_copy(out=result[:, cols], in_=res[2 * c + s])
+                else:
+                    nc.scalar.copy(out=result[:, cols], in_=res[2 * c + s])
+            nc.sync.dma_start(out=out[:, CHUNK * c + v0 : CHUNK * c + v1], in_=result[:])
+
+        compare_third(1, 0)
+        compare_third(2, 0)
+        compare_third(1, 1)
+        multiply(1, 0, 0, CHUNK)
+        multiply(2, 0, 0, CHUNK)
+        multiply(1, 1, 0, CHUNK)
+        compare_third(2, 1)
+        multiply(0, 0, 0, CHUNK)
+        store(0, 0, CHUNK)
+        multiply(2, 1, 0, CHUNK)
+        for v0 in (0, SUB):
+            multiply(0, 1, v0, v0 + SUB)
+            store(1, v0, v0 + SUB)

@@ -27,7 +27,7 @@ PASSES = K // (P * PACK)
 BANK = 512
 CHUNK = 256
 SUB = 128
-X_FIRST = 3 * T // 8
+SPARE = 96
 
 
 def tile_picked_pna_none_p_kernel(
@@ -37,6 +37,7 @@ def tile_picked_pna_none_p_kernel(
     with ExitStack() as ctx:
         lists = ctx.enter_context(tc.tile_pool(name="lists", bufs=1))
         keep = ctx.enter_context(tc.tile_pool(name="keep", bufs=1))
+        early = ctx.enter_context(tc.tile_pool(name="early", bufs=1))
         psum = ctx.enter_context(tc.psum_pool(name="psum", bufs=1))
 
         def bank(name, index):
@@ -45,35 +46,44 @@ def tile_picked_pna_none_p_kernel(
         offs_sb = lists.tile([P, S // 16], U16, name="offs_sb")
         pos_sb = [lists.tile([P, V // 16], U16, name=f"pos_sb{d}") for d in range(3)]
 
-        xs_all = keep.tile([P, T], U8, name="xs_all", align_bytes=64)
-        nc.gpsimd.memset(xs_all[:].bitcast(I32), 0)
-        ws2 = keep.tile([P, 3 * N], U8, name="ws2", align_bytes=64)
-        nc.vector.memset(ws2[:].bitcast(I32), 0)
+        xs_all = early.tile([P, T], U8, name="xs_all", offset=4096 - 256, align_bytes=64)
+        nc.gpsimd.memset(xs_all[0:SPARE, :].bitcast(I32), 0)
+        xs = [keep.tile([P, S], U8, name=f"xs{z}", align_bytes=64) for z in range(PASSES)]
+        for z in range(PASSES):
+            nc.vector.memset(xs[z][:].bitcast(I32), 0)
 
         xw_all = [keep.tile([P, T], I32, name=f"xw_all{z}", align_bytes=64) for z in range(PASSES)]
         w_rows = [w1[512 * z : 512 * (z + 1), :].rearrange("(p j) c -> p j c", j=PACK) for z in range(PASSES)]
         w_raw0 = keep.tile([P, PACK, H], F32, name="w_raw0")
-        w_raw1 = [keep.tile([P, PACK, H // 2], F32, name=f"w_raw1{i}") for i in range(2)]
 
-        def load_x(z, c0, c1):
-            nc.sync.dma_start(out=xw_all[z][:, c0:c1], in_=x_words[z].rearrange("p n t -> p (n t)").bitcast(I32)[:, c0:c1])
+        def load_x(z):
+            nc.sync.dma_start(out=xw_all[z][:], in_=x_words[z].rearrange("p n t -> p (n t)").bitcast(I32))
 
-        load_x(0, 0, X_FIRST)
+        nc.sync.dma_start(out=xs_all[SPARE:P, :].bitcast(I32), in_=x_scales.rearrange("z r c -> (z r) c").bitcast(I32))
         nc.sync.dma_start(offs_sb[:], offs)
-        for q in range(4):
-            nc.sync.dma_start(
-                out=xs_all[32 * q : 32 * q + 8, :].bitcast(I32),
-                in_=x_scales[:, 4 * q : 4 * q + 4, :].bitcast(I32),
-            )
-        load_x(0, X_FIRST, T)
-        nc.sync.dma_start(out=w_raw0[:], in_=w_rows[0])
-        load_x(1, 0, T)
-        for i in range(2):
-            nc.sync.dma_start(out=w_raw1[i][:], in_=w_rows[1][:, :, 256 * i : 256 * (i + 1)])
+        load_x(0)
         for d, pos in enumerate((pos1, pos2, pos3)):
             nc.sync.dma_start(pos_sb[d][:], pos)
+        nc.sync.dma_start(out=w_raw0[:], in_=w_rows[0])
+        load_x(1)
 
-        ww2 = [keep.tile([P, 2 * N], U8, name=f"ww2{d}", align_bytes=64) for d in range(3)]
+        picked = keep.tile([P, S], U8, name="picked", align_bytes=64)
+        nc.vector.tensor_copy(out=picked[:], in_=xs_all[:].indirect(offs_sb[:]))
+
+        def move_scales(z):
+            for q in range(4):
+                row = SPARE + 16 * z + 4 * q
+                nc.sync.dma_start(out=xs[z][32 * q : 32 * q + 4, :].bitcast(I32), in_=picked[row : row + 4, :].bitcast(I32))
+
+        w_raw1 = [early.tile([P, PACK, H // 2], F32, name=f"w_raw1{i}", offset=(0, 4096 + 1280)[i], align_bytes=64) for i in range(2)]
+        move_scales(0)
+        for i in range(2):
+            nc.sync.dma_start(out=w_raw1[i][:], in_=w_rows[1][:, :, 256 * i : 256 * (i + 1)])
+        move_scales(1)
+
+        ws2 = early.tile([P, 3 * N], U8, name="ws2", offset=4096 + 768, align_bytes=64)
+        nc.gpsimd.memset(ws2[:].bitcast(I32), 0)
+        ww2 = [early.tile([P, 2 * N], U8, name=f"ww2{d}", offset=4096 + 256 * d, align_bytes=64) for d in range(3)]
         for d, (words, scales) in enumerate(((w2_words, w2_scales), (w3_words, w3_scales), (w4_words, w4_scales))):
             nc.sync.dma_start(out=ww2[d][:].bitcast(I32), in_=words[0].bitcast(I32))
             for q in range(4):
@@ -86,7 +96,6 @@ def tile_picked_pna_none_p_kernel(
         make_identity(nc, ident[:])
 
         xw = [keep.tile([P, S], U32, name="xw0", align_bytes=64)]
-        xs = keep.tile([P, S], U8, name="xs", align_bytes=64)
         w_bf = [[keep.tile([P, 2, P, PACK], BF16, name=f"w_bf{z}{u}", tag=f"w_bf{z}{u}", align_bytes=64) for u in range(2)] for z in range(PASSES)]
         wq = [keep.tile([P, H], U32, name=f"wq{z}", align_bytes=64) for z in range(PASSES)]
         wsc = [keep.tile([P, H], U8, name=f"wsc{z}", align_bytes=64) for z in range(PASSES)]
@@ -114,7 +123,6 @@ def tile_picked_pna_none_p_kernel(
             cols = slice(P * t0, P * t1)
             nc.vector.quantize_mx(out=wq[z][:, cols].bitcast(FP8X4), scales=w_scales(z, t0, t1), in_=flat)
 
-        nc.vector.tensor_copy(out=xs[:], in_=xs_all[:].indirect(offs_sb[:]))
         nc.vector.tensor_copy(out=xw[0][:], in_=xw_all[0][:].bitcast(U32).indirect(offs_sb[:]))
         round_w_scalar(0, 0, w_raw0, 0, P)
         round_w_scalar(0, 1, w_raw0, 0, P)
@@ -139,7 +147,7 @@ def tile_picked_pna_none_p_kernel(
                 lhsT=wq[z][:, P * t : P * (t + 1)].bitcast(FP8X4),
                 lhsT_scale=w_scales(z, t, t + 1),
                 rhs=xw[z][:, c0:c1].bitcast(FP8X4),
-                rhs_scale=xs[4 * z : P, c0:c1],
+                rhs_scale=xs[z][:, c0:c1],
                 start=(z == 0),
                 stop=(z == PASSES - 1),
             )
@@ -165,7 +173,7 @@ def tile_picked_pna_none_p_kernel(
                     lhsT=wq[z][:, P * t : P * (t + 1)].bitcast(FP8X4),
                     lhsT_scale=w_scales(z, t, t + 1),
                     rhs=xw[z][:, c0 : c0 + quarter].bitcast(FP8X4),
-                    rhs_scale=xs[4 * z : P, c0 : c0 + quarter],
+                    rhs_scale=xs[z][:, c0 : c0 + quarter],
                     start=(first and e == 0),
                     stop=(last and e == 1),
                 )

@@ -54,7 +54,7 @@ def tile_picked_pna_none_p_kernel(
 
         xw_all = [keep.tile([P, T], I32, name=f"xw_all{z}", align_bytes=64) for z in range(PASSES)]
         w_rows = [w1[512 * z : 512 * (z + 1), :].rearrange("(p j) c -> p j c", j=PACK) for z in range(PASSES)]
-        w_raw0 = keep.tile([P, PACK, H], F32, name="w_raw0")
+        w_raw0 = keep.tile([P, PACK, H], F32, name="w_raw0", tag="w_raw0", align_bytes=64)
 
         def load_x(z):
             nc.sync.dma_start(out=xw_all[z][:], in_=x_words[z].rearrange("p n t -> p (n t)").bitcast(I32))
@@ -127,9 +127,16 @@ def tile_picked_pna_none_p_kernel(
         round_w_scalar(0, 0, w_raw0, 0, P)
         round_w_scalar(0, 1, w_raw0, 0, P)
         quantize_w(0, 0, 2)
-        xw.append(keep.tile([P, S], U32, name="xw1", tag="w_bf00", align_bytes=64))
-        nc.vector.tensor_copy(out=xw[1][:], in_=xw_all[1][:].bitcast(U32).indirect(offs_sb[:]))
+        late = [keep.tile([P, BANK], U32, name=f"xw1{i}", tag=("w_bf00", "w_raw0")[i], align_bytes=64) for i in range(2)]
+        nc.vector.tensor_copy(out=late[0][:], in_=xw_all[1][:].bitcast(U32).indirect(offs_sb[:, 0 : BANK // 16]))
         quantize_w(0, 2, 4)
+        nc.vector.tensor_copy(out=late[1][:], in_=xw_all[1][:].bitcast(U32).indirect(offs_sb[:, BANK // 16 : S // 16]))
+
+        def words(z, c0, c1):
+            if z == 0:
+                return xw[0][:, c0:c1].bitcast(FP8X4)
+            return late[c0 // BANK][:, c0 % BANK : c0 % BANK + c1 - c0].bitcast(FP8X4)
+
         round_w_scalar(1, 0, w_raw1[0], 0, P // 2)
         round_w_scalar(1, 1, w_raw1[0], 0, P // 2)
         round_w_scalar(1, 0, w_raw1[1], P // 2, P)
@@ -146,7 +153,7 @@ def tile_picked_pna_none_p_kernel(
                 out=acc,
                 lhsT=wq[z][:, P * t : P * (t + 1)].bitcast(FP8X4),
                 lhsT_scale=w_scales(z, t, t + 1),
-                rhs=xw[z][:, c0:c1].bitcast(FP8X4),
+                rhs=words(z, c0, c1),
                 rhs_scale=xs[z][:, c0:c1],
                 start=(z == 0),
                 stop=(z == PASSES - 1),
@@ -172,7 +179,7 @@ def tile_picked_pna_none_p_kernel(
                     out=acc[:, quarter * e : quarter * (e + 1)],
                     lhsT=wq[z][:, P * t : P * (t + 1)].bitcast(FP8X4),
                     lhsT_scale=w_scales(z, t, t + 1),
-                    rhs=xw[z][:, c0 : c0 + quarter].bitcast(FP8X4),
+                    rhs=words(z, c0, c0 + quarter),
                     rhs_scale=xs[z][:, c0 : c0 + quarter],
                     start=(first and e == 0),
                     stop=(last and e == 1),

@@ -15,9 +15,6 @@ U8 = mybir.dt.uint8
 FP8X4 = mybir.dt.float8_e4m3fn_x4
 FP4X4 = mybir.dt.float4_e2m1fn_x4
 COPY = mybir.ActivationFunctionType.Copy
-RELU = mybir.ActivationFunctionType.Relu
-ADD = mybir.AluOpType.add
-SUBTRACT = mybir.AluOpType.subtract
 MAX = mybir.AluOpType.max
 MIN = mybir.AluOpType.min
 
@@ -144,80 +141,48 @@ def tile_picked_pna_none_p_kernel(
         quantize_w(1, 0, 1)
         quantize_w(1, 1, 2)
 
-        h_first = keep.tile([P, S], F32, name="h_first", align_bytes=64)
-        h_second = keep.tile([P, S], F32, name="h_second", align_bytes=64)
-        h_rest = keep.tile([P, 2, S], F32, name="h_rest", align_bytes=64)
+        h = [keep.tile([P, S], F32, name=f"h{t}", align_bytes=64) for t in range(PACK)]
+        banks_of = ((0, 1), (2, 3), (4, 0), (1, 2))
 
-        def h_pass(acc, t, z, c0, c1):
+        def h_pass(acc, t, z, s):
             nc.tensor.matmul_mx(
-                out=acc,
+                out=acc[:],
                 lhsT=wq[z][:, P * t : P * (t + 1)].bitcast(FP8X4),
                 lhsT_scale=w_scales(z, t, t + 1),
-                rhs=words(z, c0, c1),
-                rhs_scale=xs[z][:, c0:c1],
+                rhs=words(z, BANK * s, BANK * (s + 1)),
+                rhs_scale=xs[z][:, BANK * s : BANK * (s + 1)],
                 start=(z == 0),
                 stop=(z == PASSES - 1),
             )
 
-        quarter = S // 4
-        acc = [bank(f"acc0{s}", s) for s in range(4)]
-        for z in range(PASSES):
-            for s in range(4):
-                h_pass(acc[s][:, 0:quarter], 0, z, quarter * s, quarter * (s + 1))
-        for s in range(4):
-            cols = slice(quarter * s, quarter * (s + 1))
-            if s % 2 == 0:
-                nc.vector.tensor_copy(out=h_first[:, cols], in_=acc[s][:, 0:quarter])
-            else:
-                nc.scalar.copy(out=h_first[:, cols], in_=acc[s][:, 0:quarter])
-        quantize_w(1, 2, 4)
-
-        def pair_pass(acc, z, c0, first, last):
-            for e in range(2):
-                t = 2 + e
-                nc.tensor.matmul_mx(
-                    out=acc[:, quarter * e : quarter * (e + 1)],
-                    lhsT=wq[z][:, P * t : P * (t + 1)].bitcast(FP8X4),
-                    lhsT_scale=w_scales(z, t, t + 1),
-                    rhs=words(z, c0, c0 + quarter),
-                    rhs_scale=xs[z][:, c0 : c0 + quarter],
-                    start=(first and e == 0),
-                    stop=(last and e == 1),
-                )
-
-        acc1 = [bank(f"acc1{s}", 4 + s) for s in range(2)]
-        for z in range(PASSES):
+        for t in range(PACK):
+            if t == 2:
+                quantize_w(1, 2, 4)
+            acc = [bank(f"acc{t}{s}", banks_of[t][s]) for s in range(2)]
             for s in range(2):
-                h_pass(acc1[s][:], 1, z, BANK * s, BANK * (s + 1))
-        for s in range(2):
-            nc.scalar.copy(out=h_second[:, BANK * s : BANK * (s + 1)], in_=acc1[s][:])
-        wide2, both_a, wide3, both_b = bank("wide2", 6), bank("both_a", 0), bank("wide3", 1), bank("both_b", 2)
-        for z in range(PASSES):
-            h_pass(wide2[:], 2, z, 0, BANK)
-            pair_pass(both_a, z, BANK, z == 0, z == PASSES - 1)
-        for z in range(PASSES):
-            h_pass(wide3[:], 3, z, 0, BANK)
-        for z in range(PASSES):
-            pair_pass(both_b, z, BANK + quarter, z == 0, z == PASSES - 1)
-        nc.scalar.copy(out=h_rest[:, 0, 0:BANK], in_=wide2[:])
-        nc.scalar.copy(out=h_rest[:, :, BANK : BANK + quarter], in_=both_a[:].rearrange("p (e c) -> p e c", e=2))
-        nc.scalar.copy(out=h_rest[:, 1, 0:BANK], in_=wide3[:])
-        nc.scalar.copy(out=h_rest[:, :, BANK + quarter : S], in_=both_b[:].rearrange("p (e c) -> p e c", e=2))
+                for z in range(PASSES):
+                    h_pass(acc[s], t, z, s)
+                if (t, s) == (0, 0):
+                    nc.vector.tensor_copy(out=h[t][:, BANK * s : BANK * (s + 1)], in_=acc[s][:])
+                else:
+                    nc.scalar.copy(out=h[t][:, BANK * s : BANK * (s + 1)], in_=acc[s][:])
 
         halves = V // CHUNK
         g = [[keep.tile([P, 2, V], F32, name=f"g{d}{u}", align_bytes=64) for u in range(2)] for d in range(3)]
-        gb = [keep.tile([P, V * 2], BF16, name=f"gb{d}", align_bytes=64) for d in range(2)]
-        third = [keep.tile([P, 2, CHUNK * 2], BF16, name=f"third{c}", align_bytes=64) for c in range(halves)]
+        totals = [[bank(f"total{u}{c}", ((5, 6), (7, 3))[u][c]) for c in range(halves)] for u in range(2)]
+        back = [bank(f"back{c}", (4, 0)[c]) for c in range(halves)]
+        z = [[keep.tile([P, CHUNK * PACK], BF16, name=f"z{c}{d}", align_bytes=64) for d in range(3)] for c in range(halves)]
         hi = keep.tile([P, 2, V * 2], BF16, name="hi", align_bytes=64)
         lo = keep.tile([P, 2, V * 2], BF16, name="lo", align_bytes=64)
-        totals = [[bank(f"total{u}{c}", ((3, 7), (4, 5))[u][c]) for c in range(halves)] for u in range(2)]
-        back = [bank(f"back{c}", (6, 2)[c]) for c in range(halves)]
-        z1 = [keep.tile([P, CHUNK * PACK], BF16, name=f"z1{c}", align_bytes=64) for c in range(halves)]
-        windows = [h_first[:], h_second[:], h_rest[:, 0, :], h_rest[:, 1, :]]
+        third = keep.tile([P, 2, V * 2], BF16, name="third", align_bytes=64)
 
-        def gather(d, t):
+        def gather(d, t, on_vector):
             u, e = divmod(t, 2)
-            nc.vector.tensor_copy(out=g[d][u][:, e, :], in_=windows[t].indirect(pos_sb[d][:]))
+            window = h[t][:].indirect(pos_sb[d][:])
+            if on_vector:
+                nc.vector.tensor_copy(out=g[d][u][:, e, :], in_=window)
+            else:
+                nc.scalar.activation(out=g[d][u][:, e, :], in_=window, func=COPY)
 
         def add_up(d, t, first, last):
             u, e = divmod(t, 2)
@@ -234,11 +199,23 @@ def tile_picked_pna_none_p_kernel(
                         stop=(last and s == 1),
                     )
 
-        def cast(dst, d, u, v0, v1):
-            nc.scalar.copy(
-                out=dst.rearrange("p (v i e) -> p v e i", i=4, e=2),
-                in_=g[d][u][:, :, v0:v1].rearrange("p e (v i) -> p v e i", i=4),
-            )
+        plans = [
+            [(0, 0, True), (0, 1, True), (2, 1, False), (1, 0, True), (1, 1, True), (2, 0, True)],
+            [(d, t, False) for d in range(3) for t in (2, 3)],
+        ]
+        for plan in plans:
+            for i, (d, t, on_vector) in enumerate(plan):
+                gather(d, t, on_vector)
+                add_up(d, t, i == 0, i == len(plan) - 1)
+
+        def by_rows(d, u, v0, v1):
+            return g[d][u][:, :, v0:v1].rearrange("p e (v i) -> p v e i", i=4)
+
+        def paired(tile, u, v0, v1):
+            return tile[:, u, 2 * v0 : 2 * v1].rearrange("p (v i e) -> p v e i", i=4, e=2)
+
+        def woven(tile, c):
+            return tile[:, :, CHUNK * 2 * c : CHUNK * 2 * (c + 1)].rearrange("p u (v e) -> p v u e", e=2)
 
         def turn(u, c):
             turned = keep.tile([P, 2 * P * 2], BF16, name=f"turned{u}{c}", align_bytes=64)
@@ -254,95 +231,67 @@ def tile_picked_pna_none_p_kernel(
 
         def weave(c):
             nc.scalar.copy(
-                out=z1[c][:].bitcast(F32).rearrange("p (s v u) -> p s v u", s=2, u=2),
+                out=z[c][0][:].bitcast(F32).rearrange("p (s v u) -> p s v u", s=2, u=2),
                 in_=back[c][:].rearrange("p (s u v) -> p s v u", s=2, u=2),
             )
 
-        def compare_by_difference(e):
-            a, b = g[0][0][:, e, :], g[1][0][:, e, :]
-            diff = keep.tile([P, V], F32, name=f"diff{e}", align_bytes=64)
-            excess = keep.tile([P, V], F32, name=f"excess{e}", align_bytes=64)
-            nc.gpsimd.tensor_tensor(out=diff[:], in0=a, in1=b, op=SUBTRACT)
-            nc.scalar.activation(out=excess[:], in_=diff[:], func=RELU)
-            nc.gpsimd.tensor_tensor(out=hi[:, 0, :].rearrange("p (v e) -> p v e", e=2)[:, :, e], in0=b, in1=excess[:], op=ADD)
-            nc.gpsimd.tensor_tensor(out=lo[:, 0, :].rearrange("p (v e) -> p v e", e=2)[:, :, e], in0=a, in1=excess[:], op=SUBTRACT)
+        def compare_two(tile, op, u):
+            nc.vector.tensor_tensor(out=paired(tile, u, 0, V), in0=by_rows(0, u, 0, V), in1=by_rows(1, u, 0, V), op=op)
 
-        orders = [[(d, t) for t in (0, 1) for d in range(3)], [(d, t) for d in range(3) for t in (2, 3)]]
-        for u in range(2):
-            for d, t in orders[u]:
-                gather(d, t)
-            for i, (d, t) in enumerate(orders[u]):
-                add_up(d, t, i == 0, i == len(orders[u]) - 1)
-            if u == 0:
-                compare_by_difference(0)
-                compare_by_difference(1)
-            else:
-                cast(gb[0][:], 0, u, 0, V)
-                cast(gb[1][:], 1, u, 0, V)
-            for c in range(halves):
-                cast(third[c][:, u, :], 2, u, CHUNK * c, CHUNK * (c + 1))
-            for c in range(halves):
-                turn(u, c)
-        nc.vector.tensor_tensor(out=hi[:, 1, :], in0=gb[0][:], in1=gb[1][:], op=MAX)
-        nc.vector.tensor_tensor(out=lo[:, 1, :], in0=gb[0][:], in1=gb[1][:], op=MIN)
-        for c in range(halves):
-            weave(c)
+        def round_third(u, v0, v1):
+            nc.vector.tensor_copy(out=paired(third, u, v0, v1), in_=by_rows(2, u, v0, v1))
 
-        def woven(pairs):
-            return pairs.rearrange("p u (v e) -> p v u e", e=2)
+        def compare_third(c, d):
+            tile, op = ((hi, MAX), (lo, MIN))[d - 1]
+            nc.vector.tensor_tensor(out=z[c][d][:].rearrange("p (v u e) -> p v u e", u=2, e=2), in0=woven(tile, c), in1=woven(third, c), op=op)
 
         zq = [[keep.tile([P, CHUNK], U32, name=f"zq{c}{d}", align_bytes=64) for d in range(3)] for c in range(halves)]
         zs = [[keep.tile([P, CHUNK], U8, name=f"zs{c}{d}", align_bytes=64) for d in range(3)] for c in range(halves)]
-        res = [bank(f"res{i}", (0, 1, 3, 7)[i])[:, 0:SUB] for i in range(V // SUB)]
 
-        def product(d, c, s):
-            cols = slice(SUB * s, SUB * (s + 1))
+        def quantize_z(c, d, v0, v1):
+            nc.vector.quantize_mx(out=zq[c][d][:, v0:v1].bitcast(FP8X4), scales=zs[c][d][:, v0:v1], in_=z[c][d][:, PACK * v0 : PACK * v1])
+
+        def product(res, c, d, v0, v1):
             nc.tensor.matmul_mx(
-                out=res[2 * c + s],
+                out=res[:, 0 : v1 - v0],
                 lhsT=ww2[d][:].bitcast(FP4X4),
                 lhsT_scale=ws2[:, d * N : (d + 1) * N],
-                rhs=zq[c][d][:, cols].bitcast(FP8X4),
-                rhs_scale=zs[c][d][:, cols],
+                rhs=zq[c][d][:, v0:v1].bitcast(FP8X4),
+                rhs_scale=zs[c][d][:, v0:v1],
                 start=(d == 1),
                 stop=(d == 0),
             )
 
-        z = [[z1[c]] + [keep.tile([P, CHUNK * PACK], BF16, name=f"edge{c}{d}", align_bytes=64) for d in (1, 2)] for c in range(halves)]
-
-        def compare_third(d, c):
-            two, op = ((hi, MAX), (lo, MIN))[d - 1]
-            nc.vector.tensor_tensor(
-                out=z[c][d][:].rearrange("p (v u e) -> p v u e", u=2, e=2),
-                in0=woven(two[:, :, CHUNK * 2 * c : CHUNK * 2 * (c + 1)]),
-                in1=woven(third[c][:]),
-                op=op,
-            )
-
-        def multiply(d, c, v0, v1):
-            nc.vector.quantize_mx(out=zq[c][d][:, v0:v1].bitcast(FP8X4), scales=zs[c][d][:, v0:v1], in_=z[c][d][:, PACK * v0 : PACK * v1])
-            for s in range(v0 // SUB, v1 // SUB):
-                product(d, c, s)
-
-        def store(c, v0, v1):
+        def store(res, c, v0, v1, on_vector):
             result = keep.tile([P, v1 - v0], F32, name=f"result{c}{v0}")
-            for s in range(v0 // SUB, v1 // SUB):
-                cols = slice(SUB * s - v0, SUB * (s + 1) - v0)
-                if (c, s) == (1, 1):
-                    nc.vector.tensor_copy(out=result[:, cols], in_=res[2 * c + s])
-                else:
-                    nc.scalar.copy(out=result[:, cols], in_=res[2 * c + s])
+            if on_vector:
+                nc.vector.tensor_copy(out=result[:], in_=res[:, 0 : v1 - v0])
+            else:
+                nc.scalar.copy(out=result[:], in_=res[:, 0 : v1 - v0])
             nc.sync.dma_start(out=out[:, CHUNK * c + v0 : CHUNK * c + v1], in_=result[:])
 
-        compare_third(1, 0)
-        compare_third(2, 0)
-        compare_third(1, 1)
-        multiply(1, 0, 0, CHUNK)
-        multiply(2, 0, 0, CHUNK)
-        multiply(1, 1, 0, CHUNK)
-        compare_third(2, 1)
-        multiply(0, 0, 0, CHUNK)
-        store(0, 0, CHUNK)
-        multiply(2, 1, 0, CHUNK)
-        for v0 in (0, SUB):
-            multiply(0, 1, v0, v0 + SUB)
-            store(1, v0, v0 + SUB)
+        compare_two(hi, MAX, 0)
+        round_third(0, 0, V)
+        compare_two(lo, MIN, 0)
+        compare_two(hi, MAX, 1)
+        compare_two(lo, MIN, 1)
+        for c in range(halves):
+            round_third(1, CHUNK * c, CHUNK * (c + 1))
+        for c in range(halves):
+            for d in (1, 2):
+                compare_third(c, d)
+            for d in (1, 2):
+                quantize_z(c, d, 0, CHUNK)
+        for u in range(2):
+            for c in range(halves):
+                turn(u, c)
+        for c in range(halves):
+            weave(c)
+        pieces = [(bank("res0", 1), 0, 0, CHUNK), (bank("res1", 2), 1, 0, SUB), (bank("res2", 5), 1, SUB, CHUNK)]
+        for res, c, v0, v1 in pieces:
+            for d in (1, 2):
+                product(res, c, d, v0, v1)
+        for i, (res, c, v0, v1) in enumerate(pieces):
+            quantize_z(c, 0, v0, v1)
+            product(res, c, 0, v0, v1)
+            store(res, c, v0, v1, i == len(pieces) - 1)

@@ -15,6 +15,8 @@ U8 = mybir.dt.uint8
 FP8X4 = mybir.dt.float8_e4m3fn_x4
 FP4X4 = mybir.dt.float4_e2m1fn_x4
 COPY = mybir.ActivationFunctionType.Copy
+MULT = mybir.AluOpType.mult
+ADD = mybir.AluOpType.add
 MAX = mybir.AluOpType.max
 MIN = mybir.AluOpType.min
 
@@ -162,7 +164,7 @@ def tile_picked_pna_none_p_kernel(
             for s in range(2):
                 for z in range(PASSES):
                     h_pass(acc[s], t, z, s)
-                if (t, s) == (0, 0):
+                if t < 2 and s == 0:
                     nc.vector.tensor_copy(out=h[t][:, BANK * s : BANK * (s + 1)], in_=acc[s][:])
                 else:
                     nc.scalar.copy(out=h[t][:, BANK * s : BANK * (s + 1)], in_=acc[s][:])
@@ -200,8 +202,8 @@ def tile_picked_pna_none_p_kernel(
                     )
 
         plans = [
-            [(0, 0, True), (0, 1, True), (2, 1, False), (1, 0, True), (1, 1, True), (2, 0, True)],
-            [(d, t, False) for d in range(3) for t in (2, 3)],
+            [(0, 0, True), (0, 1, True), (1, 0, False), (2, 0, True), (1, 1, False), (2, 1, True)],
+            [(0, 2, True), (1, 2, False), (0, 3, True), (1, 3, False), (2, 2, False), (2, 3, False)],
         ]
         for plan in plans:
             for i, (d, t, on_vector) in enumerate(plan):
@@ -239,7 +241,12 @@ def tile_picked_pna_none_p_kernel(
             nc.vector.tensor_tensor(out=paired(tile, u, 0, V), in0=by_rows(0, u, 0, V), in1=by_rows(1, u, 0, V), op=op)
 
         def round_third(u, v0, v1):
-            nc.vector.tensor_copy(out=paired(third, u, v0, v1), in_=by_rows(2, u, v0, v1))
+            nc.scalar.copy(out=paired(third, u, v0, v1), in_=by_rows(2, u, v0, v1))
+
+        def round_pair(dst, d):
+            nc.gpsimd.tensor_scalar(
+                out=dst.rearrange("p (v e) -> p v e", e=2), in0=g[d][0][:].rearrange("p e v -> p v e"), scalar1=1.0, scalar2=0.0, op0=MULT, op1=ADD
+            )
 
         def compare_third(c, d):
             tile, op = ((hi, MAX), (lo, MIN))[d - 1]
@@ -270,9 +277,12 @@ def tile_picked_pna_none_p_kernel(
                 nc.scalar.copy(out=result[:], in_=res[:, 0 : v1 - v0])
             nc.sync.dma_start(out=out[:, CHUNK * c + v0 : CHUNK * c + v1], in_=result[:])
 
-        compare_two(hi, MAX, 0)
-        round_third(0, 0, V)
-        compare_two(lo, MIN, 0)
+        rounded = [keep.tile([P, V * 2], BF16, name=f"rounded{d}", align_bytes=64) for d in range(2)]
+        round_pair(rounded[0][:], 0)
+        round_pair(rounded[1][:], 1)
+        round_pair(third[:, 0, :], 2)
+        nc.vector.tensor_tensor(out=hi[:, 0, :], in0=rounded[0][:], in1=rounded[1][:], op=MAX)
+        nc.vector.tensor_tensor(out=lo[:, 0, :], in0=rounded[0][:], in1=rounded[1][:], op=MIN)
         compare_two(hi, MAX, 1)
         compare_two(lo, MIN, 1)
         for c in range(halves):

@@ -45,26 +45,32 @@ def tile_picked_pna_none_p_kernel(
         offs_sb = lists.tile([P, S // 16], U16, name="offs_sb")
         pos_sb = [lists.tile([P, V // 16], U16, name=f"pos_sb{d}") for d in range(3)]
 
-        xs_all = early.tile([P, T], U8, name="xs_all", offset=4096 - 256, align_bytes=64)
+        xs_all = early.tile([P, T], U8, name="xs_all", offset=4 * T - 256, align_bytes=64)
         nc.gpsimd.memset(xs_all[0:SPARE, :].bitcast(I32), 0)
         xs = [keep.tile([P, S], U8, name=f"xs{z}", align_bytes=64) for z in range(PASSES)]
         for z in range(PASSES):
             nc.vector.memset(xs[z][:].bitcast(I32), 0)
 
-        xw_all = [keep.tile([P, T], I32, name=f"xw_all{z}", align_bytes=64) for z in range(PASSES)]
+        xw_all = [keep.tile([P, T], I32, name="xw_all0", align_bytes=64), early.tile([P, T], I32, name="xw_all1", offset=0, align_bytes=64)]
         w_rows = [w1[512 * z : 512 * (z + 1), :].rearrange("(p j) c -> p j c", j=PACK) for z in range(PASSES)]
         w_raw0 = keep.tile([P, PACK, H], F32, name="w_raw0", tag="w_raw0", align_bytes=64)
+        cuts = (0, H // 4, H // 2, H)
+        w_late = early.tile([P, PACK * (H - cuts[1])], F32, name="w_late", offset=4 * T + 1280, align_bytes=64)
+        w_raw1 = [keep.tile([P, PACK, cuts[1]], F32, name="w_raw10", align_bytes=64)[:]] + [
+            w_late[:, PACK * (cuts[i] - cuts[1]) : PACK * (cuts[i + 1] - cuts[1])].rearrange("p (j c) -> p j c", j=PACK) for i in (1, 2)
+        ]
 
         def load_x(z):
             nc.sync.dma_start(out=xw_all[z][:], in_=x_words[z].rearrange("p n t -> p (n t)").bitcast(I32))
 
+        def load_w1(i):
+            nc.sync.dma_start(out=w_raw1[i], in_=w_rows[1][:, :, cuts[i] : cuts[i + 1]])
+
         nc.sync.dma_start(out=xs_all[SPARE:P, :].bitcast(I32), in_=x_scales.rearrange("z r c -> (z r) c").bitcast(I32))
         nc.sync.dma_start(offs_sb[:], offs)
         load_x(0)
-        for d, pos in enumerate((pos1, pos2, pos3)):
-            nc.sync.dma_start(pos_sb[d][:], pos)
         nc.sync.dma_start(out=w_raw0[:], in_=w_rows[0])
-        load_x(1)
+        load_w1(0)
 
         picked = keep.tile([P, S], U8, name="picked", align_bytes=64)
         nc.vector.tensor_copy(out=picked[:], in_=xs_all[:].indirect(offs_sb[:]))
@@ -74,15 +80,17 @@ def tile_picked_pna_none_p_kernel(
                 row = SPARE + 16 * z + 4 * q
                 nc.sync.dma_start(out=xs[z][32 * q : 32 * q + 4, :].bitcast(I32), in_=picked[row : row + 4, :].bitcast(I32))
 
-        w_raw1 = [early.tile([P, PACK, H // 2], F32, name=f"w_raw1{i}", offset=(0, 4096 + 1280)[i], align_bytes=64) for i in range(2)]
         move_scales(0)
-        for i in range(2):
-            nc.sync.dma_start(out=w_raw1[i][:], in_=w_rows[1][:, :, 256 * i : 256 * (i + 1)])
+        load_x(1)
+        load_w1(1)
+        load_w1(2)
         move_scales(1)
+        for d, pos in enumerate((pos1, pos2, pos3)):
+            nc.sync.dma_start(pos_sb[d][:], pos)
 
-        ws2 = early.tile([P, 3 * N], U8, name="ws2", offset=4096 + 768, align_bytes=64)
+        ws2 = early.tile([P, 3 * N], U8, name="ws2", offset=4 * T + 768, align_bytes=64)
         nc.gpsimd.memset(ws2[:].bitcast(I32), 0)
-        ww2 = [early.tile([P, 2 * N], U8, name=f"ww2{d}", offset=4096 + 256 * d, align_bytes=64) for d in range(3)]
+        ww2 = [early.tile([P, 2 * N], U8, name=f"ww2{d}", offset=4 * T + 256 * d, align_bytes=64) for d in range(3)]
         for d, (words, scales) in enumerate(((w2_words, w2_scales), (w3_words, w3_scales), (w4_words, w4_scales))):
             nc.sync.dma_start(out=ww2[d][:].bitcast(I32), in_=words[0].bitcast(I32))
             for q in range(4):
@@ -103,7 +111,7 @@ def tile_picked_pna_none_p_kernel(
             r0 = m0 if z == 0 else 0
             return (
                 w_bf[z][u][:, :, m0:m1, :].rearrange("p e m j -> p m j e"),
-                raw[:].rearrange("p j (m t) -> p m j t", t=PACK)[:, r0 : r0 + m1 - m0, :, 2 * u : 2 * u + 2],
+                raw.rearrange("p j (m t) -> p m j t", t=PACK)[:, r0 : r0 + m1 - m0, :, 2 * u : 2 * u + 2],
             )
 
         def round_w_scalar(*args):
@@ -111,11 +119,7 @@ def tile_picked_pna_none_p_kernel(
             nc.scalar.activation(out=dst, in_=src, func=COPY)
 
         def w_scales(z, t0, t1):
-            if z == 0:
-                return wsc[z][:, P * t0 : P * t1]
-            if t0 >= 2:
-                return wsc[z][4:P, P * (t0 - 2) : P * (t1 - 2)]
-            return wsc[z][:, 2 * P * t0 : 2 * P * t0 + P]
+            return wsc[z][:, P * t0 : P * t1]
 
         def quantize_w(z, t0, t1):
             flat = w_bf[z][t0 // 2][:, t0 % 2 : t0 % 2 + t1 - t0, :, :].rearrange("p e m j -> p (e m j)")
@@ -123,28 +127,26 @@ def tile_picked_pna_none_p_kernel(
             nc.vector.quantize_mx(out=wq[z][:, cols].bitcast(FP8X4), scales=w_scales(z, t0, t1), in_=flat)
 
         nc.vector.tensor_copy(out=xw[0][:], in_=xw_all[0][:].bitcast(U32).indirect(offs_sb[:]))
-        round_w_scalar(0, 0, w_raw0, 0, P)
-        round_w_scalar(0, 1, w_raw0, 0, P)
+        dst, src = w_views(0, 0, w_raw0[:], 0, P)
+        nc.vector.tensor_copy(out=dst, in_=src)
+        round_w_scalar(0, 1, w_raw0[:], 0, P)
         quantize_w(0, 0, 2)
-        late = [keep.tile([P, BANK], U32, name=f"xw1{i}", tag=("w_bf00", "w_raw0")[i], align_bytes=64) for i in range(2)]
-        nc.vector.tensor_copy(out=late[0][:], in_=xw_all[1][:].bitcast(U32).indirect(offs_sb[:, 0 : BANK // 16]))
         quantize_w(0, 2, 4)
-        nc.vector.tensor_copy(out=late[1][:], in_=xw_all[1][:].bitcast(U32).indirect(offs_sb[:, BANK // 16 : S // 16]))
+        xw.append(keep.tile([P, S], U32, name="xw1", tag="w_bf01", align_bytes=64))
+        nc.vector.tensor_copy(out=xw[1][:], in_=xw_all[1][:].bitcast(U32).indirect(offs_sb[:]))
 
         def words(z, c0, c1):
-            if z == 0:
-                return xw[0][:, c0:c1].bitcast(FP8X4)
-            return late[c0 // BANK][:, c0 % BANK : c0 % BANK + c1 - c0].bitcast(FP8X4)
+            return xw[z][:, c0:c1].bitcast(FP8X4)
 
-        round_w_scalar(1, 0, w_raw1[0], 0, P // 2)
-        round_w_scalar(1, 1, w_raw1[0], 0, P // 2)
-        round_w_scalar(1, 0, w_raw1[1], P // 2, P)
-        round_w_scalar(1, 1, w_raw1[1], P // 2, P)
-        quantize_w(1, 0, 1)
+        for i in range(3):
+            for u in range(2):
+                round_w_scalar(1, u, w_raw1[i], cuts[i] // PACK, cuts[i + 1] // PACK)
         quantize_w(1, 1, 2)
+        quantize_w(1, 0, 1)
+        quantize_w(1, 2, 4)
 
         h = [keep.tile([P, S], F32, name=f"h{t}", align_bytes=64) for t in range(PACK)]
-        banks_of = ((0, 1), (2, 3), (4, 0), (1, 2))
+        banks_of = ((0, 1), (2, 3), (4, 5), (6, 7))
 
         def h_pass(acc, t, z, s):
             nc.tensor.matmul_mx(
@@ -157,26 +159,31 @@ def tile_picked_pna_none_p_kernel(
                 stop=(z == PASSES - 1),
             )
 
-        for t in range(PACK):
-            if t == 2:
-                quantize_w(1, 2, 4)
-            acc = [bank(f"acc{t}{s}", banks_of[t][s]) for s in range(2)]
-            for s in range(2):
-                for z in range(PASSES):
-                    h_pass(acc[s], t, z, s)
-                if t < 2 and s == 0:
-                    nc.vector.tensor_copy(out=h[t][:, BANK * s : BANK * (s + 1)], in_=acc[s][:])
-                else:
-                    nc.scalar.copy(out=h[t][:, BANK * s : BANK * (s + 1)], in_=acc[s][:])
+        accs = [[bank(f"acc{t}{s}", banks_of[t][s]) for s in range(2)] for t in range(PACK)]
+        def make_h(t, s):
+            for z in range(PASSES):
+                h_pass(accs[t][s], t, z, s)
+
+        def empty_h(t, s, on_vector):
+            if on_vector:
+                nc.vector.tensor_copy(out=h[t][:, BANK * s : BANK * (s + 1)], in_=accs[t][s][:])
+            else:
+                nc.scalar.copy(out=h[t][:, BANK * s : BANK * (s + 1)], in_=accs[t][s][:])
+
+        for i, (t, s) in enumerate(((1, 0), (0, 0), (0, 1), (1, 1))):
+            make_h(t, s)
+            empty_h(t, s, i % 2 == 1)
+        later = [(t, s) for t in (2, 3) for s in range(2)]
+        for t, s in later:
+            make_h(t, s)
 
         halves = V // CHUNK
-        g = [[keep.tile([P, 2, V], F32, name=f"g{d}{u}", align_bytes=64) for u in range(2)] for d in range(3)]
-        totals = [[bank(f"total{u}{c}", ((5, 6), (7, 3))[u][c]) for c in range(halves)] for u in range(2)]
-        back = [bank(f"back{c}", (4, 0)[c]) for c in range(halves)]
+        g = [[keep.tile([P, 2, V], F32, name=f"g{d}{u}", tag=f"g{d}{u}", align_bytes=64) for u in range(2)] for d in range(3)]
+        totals = [[bank(f"total{u}{c}", ((0, 1), (2, 3))[u][c]) for c in range(halves)] for u in range(2)]
+        back = [bank(f"back{c}", (4, 5)[c]) for c in range(halves)]
         z = [[keep.tile([P, CHUNK * PACK], BF16, name=f"z{c}{d}", align_bytes=64) for d in range(3)] for c in range(halves)]
         hi = keep.tile([P, 2, V * 2], BF16, name="hi", align_bytes=64)
         lo = keep.tile([P, 2, V * 2], BF16, name="lo", align_bytes=64)
-        third = keep.tile([P, 2, V * 2], BF16, name="third", align_bytes=64)
 
         def gather(d, t, on_vector):
             u, e = divmod(t, 2)
@@ -202,10 +209,13 @@ def tile_picked_pna_none_p_kernel(
                     )
 
         plans = [
-            [(0, 0, True), (0, 1, True), (1, 0, False), (2, 0, True), (1, 1, False), (2, 1, True)],
-            [(0, 2, True), (1, 2, False), (0, 3, True), (1, 3, False), (2, 2, False), (2, 3, False)],
+            [(0, 0, True), (0, 1, False), (1, 0, True), (1, 1, False), (2, 0, True), (2, 1, True)],
+            [(0, 2, True), (0, 3, False), (1, 2, True), (1, 3, False), (2, 2, False), (2, 3, False)],
         ]
-        for plan in plans:
+        for u, plan in enumerate(plans):
+            if u == 1:
+                for t, s in later:
+                    empty_h(t, s, False)
             for i, (d, t, on_vector) in enumerate(plan):
                 gather(d, t, on_vector)
                 add_up(d, t, i == 0, i == len(plan) - 1)
@@ -231,10 +241,10 @@ def tile_picked_pna_none_p_kernel(
             for s in range(2):
                 nc.tensor.transpose(back[c][:, P * (2 * s + u) : P * (2 * s + u + 1)], pairs[:, P * s : P * (s + 1)], ident[:])
 
-        def weave(c):
+        def weave(c, s0, s1):
             nc.scalar.copy(
-                out=z[c][0][:].bitcast(F32).rearrange("p (s v u) -> p s v u", s=2, u=2),
-                in_=back[c][:].rearrange("p (s u v) -> p s v u", s=2, u=2),
+                out=z[c][0][:, PACK * SUB * s0 : PACK * SUB * s1].bitcast(F32).rearrange("p (s v u) -> p s v u", v=SUB, u=2),
+                in_=back[c][:, 2 * SUB * s0 : 2 * SUB * s1].rearrange("p (s u v) -> p s v u", v=SUB, u=2),
             )
 
         def compare_two(tile, op, u):
@@ -277,7 +287,8 @@ def tile_picked_pna_none_p_kernel(
                 nc.scalar.copy(out=result[:], in_=res[:, 0 : v1 - v0])
             nc.sync.dma_start(out=out[:, CHUNK * c + v0 : CHUNK * c + v1], in_=result[:])
 
-        rounded = [keep.tile([P, V * 2], BF16, name=f"rounded{d}", align_bytes=64) for d in range(2)]
+        rounded = [keep.tile([P, V * 2], BF16, name=f"rounded{d}", tag=("rounded0", "g00")[d], align_bytes=64) for d in range(2)]
+        third = keep.tile([P, 2, V * 2], BF16, name="third", tag="g10", align_bytes=64)
         round_pair(rounded[0][:], 0)
         round_pair(rounded[1][:], 1)
         round_pair(third[:, 0, :], 2)
@@ -295,9 +306,10 @@ def tile_picked_pna_none_p_kernel(
         for u in range(2):
             for c in range(halves):
                 turn(u, c)
-        for c in range(halves):
-            weave(c)
-        pieces = [(bank("res0", 1), 0, 0, CHUNK), (bank("res1", 2), 1, 0, SUB), (bank("res2", 5), 1, SUB, CHUNK)]
+        weave(0, 0, 2)
+        weave(1, 0, 1)
+        weave(1, 1, 2)
+        pieces = [(bank("res0", 6), 0, 0, CHUNK), (bank("res1", 7), 1, 0, SUB), (bank("res2", 0), 1, SUB, CHUNK)]
         for res, c, v0, v1 in pieces:
             for d in (1, 2):
                 product(res, c, d, v0, v1)

@@ -45,32 +45,26 @@ def tile_picked_pna_none_p_kernel(
         offs_sb = lists.tile([P, S // 16], U16, name="offs_sb")
         pos_sb = [lists.tile([P, V // 16], U16, name=f"pos_sb{d}") for d in range(3)]
 
-        xs_all = early.tile([P, T], U8, name="xs_all", offset=4 * T - 256, align_bytes=64)
+        xs_all = early.tile([P, T], U8, name="xs_all", offset=4096 - 256, align_bytes=64)
         nc.gpsimd.memset(xs_all[0:SPARE, :].bitcast(I32), 0)
         xs = [keep.tile([P, S], U8, name=f"xs{z}", align_bytes=64) for z in range(PASSES)]
         for z in range(PASSES):
             nc.vector.memset(xs[z][:].bitcast(I32), 0)
 
-        xw_all = [keep.tile([P, T], I32, name="xw_all0", align_bytes=64), early.tile([P, T], I32, name="xw_all1", offset=0, align_bytes=64)]
+        xw_all = [keep.tile([P, T], I32, name=f"xw_all{z}", align_bytes=64) for z in range(PASSES)]
         w_rows = [w1[512 * z : 512 * (z + 1), :].rearrange("(p j) c -> p j c", j=PACK) for z in range(PASSES)]
         w_raw0 = keep.tile([P, PACK, H], F32, name="w_raw0", tag="w_raw0", align_bytes=64)
-        cuts = (0, H // 4, H // 2, H)
-        w_late = early.tile([P, PACK * (H - cuts[1])], F32, name="w_late", offset=4 * T + 1280, align_bytes=64)
-        w_raw1 = [keep.tile([P, PACK, cuts[1]], F32, name="w_raw10", align_bytes=64)[:]] + [
-            w_late[:, PACK * (cuts[i] - cuts[1]) : PACK * (cuts[i + 1] - cuts[1])].rearrange("p (j c) -> p j c", j=PACK) for i in (1, 2)
-        ]
 
         def load_x(z):
             nc.sync.dma_start(out=xw_all[z][:], in_=x_words[z].rearrange("p n t -> p (n t)").bitcast(I32))
 
-        def load_w1(i):
-            nc.sync.dma_start(out=w_raw1[i], in_=w_rows[1][:, :, cuts[i] : cuts[i + 1]])
-
         nc.sync.dma_start(out=xs_all[SPARE:P, :].bitcast(I32), in_=x_scales.rearrange("z r c -> (z r) c").bitcast(I32))
         nc.sync.dma_start(offs_sb[:], offs)
         load_x(0)
+        for d, pos in enumerate((pos1, pos2, pos3)):
+            nc.sync.dma_start(pos_sb[d][:], pos)
         nc.sync.dma_start(out=w_raw0[:], in_=w_rows[0])
-        load_w1(0)
+        load_x(1)
 
         picked = keep.tile([P, S], U8, name="picked", align_bytes=64)
         nc.vector.tensor_copy(out=picked[:], in_=xs_all[:].indirect(offs_sb[:]))
@@ -80,17 +74,15 @@ def tile_picked_pna_none_p_kernel(
                 row = SPARE + 16 * z + 4 * q
                 nc.sync.dma_start(out=xs[z][32 * q : 32 * q + 4, :].bitcast(I32), in_=picked[row : row + 4, :].bitcast(I32))
 
+        w_raw1 = [early.tile([P, PACK, H // 2], F32, name=f"w_raw1{i}", offset=(0, 4096 + 1280)[i], align_bytes=64) for i in range(2)]
         move_scales(0)
-        load_x(1)
-        load_w1(1)
-        load_w1(2)
+        for i in range(2):
+            nc.sync.dma_start(out=w_raw1[i][:], in_=w_rows[1][:, :, 256 * i : 256 * (i + 1)])
         move_scales(1)
-        for d, pos in enumerate((pos1, pos2, pos3)):
-            nc.sync.dma_start(pos_sb[d][:], pos)
 
-        ws2 = early.tile([P, 3 * N], U8, name="ws2", offset=4 * T + 768, align_bytes=64)
+        ws2 = early.tile([P, 3 * N], U8, name="ws2", offset=4096 + 768, align_bytes=64)
         nc.gpsimd.memset(ws2[:].bitcast(I32), 0)
-        ww2 = [early.tile([P, 2 * N], U8, name=f"ww2{d}", offset=4 * T + 256 * d, align_bytes=64) for d in range(3)]
+        ww2 = [early.tile([P, 2 * N], U8, name=f"ww2{d}", offset=4096 + 256 * d, align_bytes=64) for d in range(3)]
         for d, (words, scales) in enumerate(((w2_words, w2_scales), (w3_words, w3_scales), (w4_words, w4_scales))):
             nc.sync.dma_start(out=ww2[d][:].bitcast(I32), in_=words[0].bitcast(I32))
             for q in range(4):
@@ -111,7 +103,7 @@ def tile_picked_pna_none_p_kernel(
             r0 = m0 if z == 0 else 0
             return (
                 w_bf[z][u][:, :, m0:m1, :].rearrange("p e m j -> p m j e"),
-                raw.rearrange("p j (m t) -> p m j t", t=PACK)[:, r0 : r0 + m1 - m0, :, 2 * u : 2 * u + 2],
+                raw[:].rearrange("p j (m t) -> p m j t", t=PACK)[:, r0 : r0 + m1 - m0, :, 2 * u : 2 * u + 2],
             )
 
         def round_w_scalar(*args):
@@ -127,26 +119,29 @@ def tile_picked_pna_none_p_kernel(
             nc.vector.quantize_mx(out=wq[z][:, cols].bitcast(FP8X4), scales=w_scales(z, t0, t1), in_=flat)
 
         nc.vector.tensor_copy(out=xw[0][:], in_=xw_all[0][:].bitcast(U32).indirect(offs_sb[:]))
-        dst, src = w_views(0, 0, w_raw0[:], 0, P)
-        nc.vector.tensor_copy(out=dst, in_=src)
-        round_w_scalar(0, 1, w_raw0[:], 0, P)
+        round_w_scalar(0, 0, w_raw0, 0, P)
+        round_w_scalar(0, 1, w_raw0, 0, P)
         quantize_w(0, 0, 2)
+        late = [keep.tile([P, BANK], U32, name=f"xw1{i}", tag=("w_bf00", "w_raw0")[i], align_bytes=64) for i in range(2)]
+        nc.vector.tensor_copy(out=late[0][:], in_=xw_all[1][:].bitcast(U32).indirect(offs_sb[:, 0 : BANK // 16]))
         quantize_w(0, 2, 4)
-        xw.append(keep.tile([P, S], U32, name="xw1", tag="w_bf01", align_bytes=64))
-        nc.vector.tensor_copy(out=xw[1][:], in_=xw_all[1][:].bitcast(U32).indirect(offs_sb[:]))
+        nc.vector.tensor_copy(out=late[1][:], in_=xw_all[1][:].bitcast(U32).indirect(offs_sb[:, BANK // 16 : S // 16]))
 
         def words(z, c0, c1):
-            return xw[z][:, c0:c1].bitcast(FP8X4)
+            if z == 0:
+                return xw[0][:, c0:c1].bitcast(FP8X4)
+            return late[c0 // BANK][:, c0 % BANK : c0 % BANK + c1 - c0].bitcast(FP8X4)
 
-        for i in range(3):
-            for u in range(2):
-                round_w_scalar(1, u, w_raw1[i], cuts[i] // PACK, cuts[i + 1] // PACK)
+        round_w_scalar(1, 0, w_raw1[0], 0, P // 2)
+        round_w_scalar(1, 1, w_raw1[0], 0, P // 2)
+        round_w_scalar(1, 0, w_raw1[1], P // 2, P)
+        round_w_scalar(1, 1, w_raw1[1], P // 2, P)
         quantize_w(1, 1, 2)
         quantize_w(1, 0, 1)
         quantize_w(1, 2, 4)
 
         h = [keep.tile([P, S], F32, name=f"h{t}", align_bytes=64) for t in range(PACK)]
-        banks_of = ((0, 1), (2, 3), (4, 5), (6, 7))
+        banks_of = ((1, 2), (0, 3), (4, 0), (1, 2))
 
         def h_pass(acc, t, z, s):
             nc.tensor.matmul_mx(
@@ -159,16 +154,17 @@ def tile_picked_pna_none_p_kernel(
                 stop=(z == PASSES - 1),
             )
 
-        accs = [[bank(f"acc{t}{s}", banks_of[t][s]) for s in range(2)] for t in range(PACK)]
+        accs = {}
         def make_h(t, s):
+            accs[t, s] = bank(f"acc{t}{s}", banks_of[t][s])
             for z in range(PASSES):
-                h_pass(accs[t][s], t, z, s)
+                h_pass(accs[t, s], t, z, s)
 
         def empty_h(t, s, on_vector):
             if on_vector:
-                nc.vector.tensor_copy(out=h[t][:, BANK * s : BANK * (s + 1)], in_=accs[t][s][:])
+                nc.vector.tensor_copy(out=h[t][:, BANK * s : BANK * (s + 1)], in_=accs[t, s][:])
             else:
-                nc.scalar.copy(out=h[t][:, BANK * s : BANK * (s + 1)], in_=accs[t][s][:])
+                nc.scalar.copy(out=h[t][:, BANK * s : BANK * (s + 1)], in_=accs[t, s][:])
 
         for i, (t, s) in enumerate(((1, 0), (0, 0), (0, 1), (1, 1))):
             make_h(t, s)
@@ -179,46 +175,47 @@ def tile_picked_pna_none_p_kernel(
 
         halves = V // CHUNK
         g = [[keep.tile([P, 2, V], F32, name=f"g{d}{u}", tag=f"g{d}{u}", align_bytes=64) for u in range(2)] for d in range(3)]
-        totals = [[bank(f"total{u}{c}", ((0, 1), (2, 3))[u][c]) for c in range(halves)] for u in range(2)]
-        back = [bank(f"back{c}", (4, 5)[c]) for c in range(halves)]
+        totals = [[bank(f"total{u}{c}", ((5, 6), (7, 3))[u][c]) for c in range(halves)] for u in range(2)]
+        back = [bank(f"back{c}", (4, 0)[c]) for c in range(halves)]
         z = [[keep.tile([P, CHUNK * PACK], BF16, name=f"z{c}{d}", align_bytes=64) for d in range(3)] for c in range(halves)]
         hi = keep.tile([P, 2, V * 2], BF16, name="hi", align_bytes=64)
         lo = keep.tile([P, 2, V * 2], BF16, name="lo", align_bytes=64)
 
-        def gather(d, t, on_vector):
+        def gather(d, t, c0, c1, on_vector):
             u, e = divmod(t, 2)
-            window = h[t][:].indirect(pos_sb[d][:])
+            window = h[t][:].indirect(pos_sb[d][:, CHUNK // 16 * c0 : CHUNK // 16 * c1])
             if on_vector:
-                nc.vector.tensor_copy(out=g[d][u][:, e, :], in_=window)
+                nc.vector.tensor_copy(out=g[d][u][:, e, CHUNK * c0 : CHUNK * c1], in_=window)
             else:
-                nc.scalar.activation(out=g[d][u][:, e, :], in_=window, func=COPY)
+                nc.scalar.activation(out=g[d][u][:, e, CHUNK * c0 : CHUNK * c1], in_=window, func=COPY)
 
-        def add_up(d, t, first, last):
+        def add_up(d, t, c, first, last):
             u, e = divmod(t, 2)
-            for c in range(halves):
-                for s in range(2):
-                    v0 = CHUNK * c + SUB * s
-                    col = P * (2 * s + e)
-                    nc.tensor.matmul(
-                        totals[u][c][:, col : col + P],
-                        lhsT=g[d][u][:, e, v0 : v0 + SUB],
-                        rhs=ident[:],
-                        is_transpose=True,
-                        start=(first and s == 0),
-                        stop=(last and s == 1),
-                    )
+            for s in range(2):
+                v0 = CHUNK * c + SUB * s
+                col = P * (2 * s + e)
+                nc.tensor.matmul(
+                    totals[u][c][:, col : col + P],
+                    lhsT=g[d][u][:, e, v0 : v0 + SUB],
+                    rhs=ident[:],
+                    is_transpose=True,
+                    start=(first and s == 0),
+                    stop=(last and s == 1),
+                )
 
         plans = [
-            [(0, 0, True), (0, 1, False), (1, 0, True), (1, 1, False), (2, 0, True), (2, 1, True)],
-            [(0, 2, True), (0, 3, False), (1, 2, True), (1, 3, False), (2, 2, False), (2, 3, False)],
+            [(0, 0, 0, 2, True), (0, 1, 0, 2, False), (1, 0, 0, 2, True), (1, 1, 0, 2, False), (2, 0, 0, 2, True), (2, 1, 0, 2, True)],
+            [(2, 2, 0, 1, True), (2, 3, 0, 1, True), (0, 2, 0, 2, False), (0, 3, 0, 2, True), (1, 2, 0, 2, False), (1, 3, 0, 2, False), (2, 2, 1, 2, False), (2, 3, 1, 2, False)],
         ]
         for u, plan in enumerate(plans):
             if u == 1:
                 for t, s in later:
                     empty_h(t, s, False)
-            for i, (d, t, on_vector) in enumerate(plan):
-                gather(d, t, on_vector)
-                add_up(d, t, i == 0, i == len(plan) - 1)
+            for i, (d, t, c0, c1, on_vector) in enumerate(plan):
+                gather(d, t, c0, c1, on_vector)
+                for c in range(c0, c1):
+                    steps = [j for j, step in enumerate(plan) if step[2] <= c < step[3]]
+                    add_up(d, t, c, i == steps[0], i == steps[-1])
 
         def by_rows(d, u, v0, v1):
             return g[d][u][:, :, v0:v1].rearrange("p e (v i) -> p v e i", i=4)
@@ -253,9 +250,9 @@ def tile_picked_pna_none_p_kernel(
         def round_third(u, v0, v1):
             nc.scalar.copy(out=paired(third, u, v0, v1), in_=by_rows(2, u, v0, v1))
 
-        def round_pair(dst, d):
+        def round_pair(dst, d, u, v0, v1):
             nc.gpsimd.tensor_scalar(
-                out=dst.rearrange("p (v e) -> p v e", e=2), in0=g[d][0][:].rearrange("p e v -> p v e"), scalar1=1.0, scalar2=0.0, op0=MULT, op1=ADD
+                out=dst.rearrange("p (v e) -> p v e", e=2), in0=g[d][u][:, :, v0:v1].rearrange("p e v -> p v e"), scalar1=1.0, scalar2=0.0, op0=MULT, op1=ADD
             )
 
         def compare_third(c, d):
@@ -289,15 +286,15 @@ def tile_picked_pna_none_p_kernel(
 
         rounded = [keep.tile([P, V * 2], BF16, name=f"rounded{d}", tag=("rounded0", "g00")[d], align_bytes=64) for d in range(2)]
         third = keep.tile([P, 2, V * 2], BF16, name="third", tag="g10", align_bytes=64)
-        round_pair(rounded[0][:], 0)
-        round_pair(rounded[1][:], 1)
-        round_pair(third[:, 0, :], 2)
+        round_pair(rounded[0][:], 0, 0, 0, V)
+        round_pair(rounded[1][:], 1, 0, 0, V)
+        round_pair(third[:, 0, :], 2, 0, 0, V)
+        round_pair(third[:, 1, 0 : 2 * CHUNK], 2, 1, 0, CHUNK)
         nc.vector.tensor_tensor(out=hi[:, 0, :], in0=rounded[0][:], in1=rounded[1][:], op=MAX)
         nc.vector.tensor_tensor(out=lo[:, 0, :], in0=rounded[0][:], in1=rounded[1][:], op=MIN)
         compare_two(hi, MAX, 1)
         compare_two(lo, MIN, 1)
-        for c in range(halves):
-            round_third(1, CHUNK * c, CHUNK * (c + 1))
+        round_third(1, CHUNK, V)
         for c in range(halves):
             for d in (1, 2):
                 compare_third(c, d)
@@ -309,7 +306,7 @@ def tile_picked_pna_none_p_kernel(
         weave(0, 0, 2)
         weave(1, 0, 1)
         weave(1, 1, 2)
-        pieces = [(bank("res0", 6), 0, 0, CHUNK), (bank("res1", 7), 1, 0, SUB), (bank("res2", 0), 1, SUB, CHUNK)]
+        pieces = [(bank("res0", 1), 0, 0, CHUNK), (bank("res1", 2), 1, 0, SUB), (bank("res2", 5), 1, SUB, CHUNK)]
         for res, c, v0, v1 in pieces:
             for d in (1, 2):
                 product(res, c, d, v0, v1)

@@ -135,13 +135,22 @@ def tile_picked_pna_none_p_kernel(
         round_w_scalar(1, 0, w_raw1[0], 0, P // 2)
         round_w_scalar(1, 1, w_raw1[0], 0, P // 2)
         round_w_scalar(1, 0, w_raw1[1], P // 2, P)
-        round_w_scalar(1, 1, w_raw1[1], P // 2, P)
-        quantize_w(1, 1, 2)
+        dst, src = w_views(1, 1, w_raw1[1], P // 2, P)
+        nc.scalar.activation(out=dst[:, 0 : P // 4], in_=src[:, 0 : P // 4], func=COPY)
+        nc.gpsimd.tensor_scalar(
+            out=dst[:, P // 4 : P // 2].rearrange("p m j e -> p e m j"),
+            in0=src[:, P // 4 : P // 2].rearrange("p m j e -> p e m j"),
+            scalar1=1.0,
+            scalar2=0.0,
+            op0=MULT,
+            op1=ADD,
+        )
         quantize_w(1, 0, 1)
+        quantize_w(1, 1, 2)
         quantize_w(1, 2, 4)
 
         h = [keep.tile([P, S], F32, name=f"h{t}", align_bytes=64) for t in range(PACK)]
-        banks_of = ((1, 2), (0, 3), (4, 0), (1, 2))
+        banks_of = ((0, 1), (2, 3), (4, 0), (1, 2))
 
         def h_pass(acc, t, z, s):
             nc.tensor.matmul_mx(
@@ -166,9 +175,9 @@ def tile_picked_pna_none_p_kernel(
             else:
                 nc.scalar.copy(out=h[t][:, BANK * s : BANK * (s + 1)], in_=accs[t, s][:])
 
-        for i, (t, s) in enumerate(((1, 0), (0, 0), (0, 1), (1, 1))):
+        for t, s in ((0, 0), (0, 1), (1, 0), (1, 1)):
             make_h(t, s)
-            empty_h(t, s, i % 2 == 1)
+            empty_h(t, s, s == 0)
         later = [(t, s) for t in (2, 3) for s in range(2)]
         for t, s in later:
             make_h(t, s)
@@ -205,7 +214,7 @@ def tile_picked_pna_none_p_kernel(
 
         plans = [
             [(0, 0, 0, 2, True), (0, 1, 0, 2, False), (1, 0, 0, 2, True), (1, 1, 0, 2, False), (2, 0, 0, 2, True), (2, 1, 0, 2, True)],
-            [(2, 2, 0, 1, True), (2, 3, 0, 1, True), (0, 2, 0, 2, False), (0, 3, 0, 2, True), (1, 2, 0, 2, False), (1, 3, 0, 2, False), (2, 2, 1, 2, False), (2, 3, 1, 2, False)],
+            [(2, 2, 0, 1, True), (2, 3, 0, 1, True), (0, 2, 0, 2, False), (0, 3, 0, 2, True), (1, 2, 0, 1, False), (1, 3, 0, 1, False), (1, 2, 1, 2, False), (1, 3, 1, 2, False), (2, 2, 1, 2, False), (2, 3, 1, 2, False)],
         ]
         for u, plan in enumerate(plans):
             if u == 1:
@@ -244,8 +253,9 @@ def tile_picked_pna_none_p_kernel(
                 in_=back[c][:, 2 * SUB * s0 : 2 * SUB * s1].rearrange("p (s u v) -> p s v u", v=SUB, u=2),
             )
 
-        def compare_two(tile, op, u):
-            nc.vector.tensor_tensor(out=paired(tile, u, 0, V), in0=by_rows(0, u, 0, V), in1=by_rows(1, u, 0, V), op=op)
+        def compare_two(tile, op, u, c):
+            v0, v1 = CHUNK * c, CHUNK * (c + 1)
+            nc.vector.tensor_tensor(out=paired(tile, u, v0, v1), in0=by_rows(0, u, v0, v1), in1=by_rows(1, u, v0, v1), op=op)
 
         def round_third(u, v0, v1):
             nc.scalar.copy(out=paired(third, u, v0, v1), in_=by_rows(2, u, v0, v1))
@@ -292,8 +302,9 @@ def tile_picked_pna_none_p_kernel(
         round_pair(third[:, 1, 0 : 2 * CHUNK], 2, 1, 0, CHUNK)
         nc.vector.tensor_tensor(out=hi[:, 0, :], in0=rounded[0][:], in1=rounded[1][:], op=MAX)
         nc.vector.tensor_tensor(out=lo[:, 0, :], in0=rounded[0][:], in1=rounded[1][:], op=MIN)
-        compare_two(hi, MAX, 1)
-        compare_two(lo, MIN, 1)
+        for c in range(halves):
+            compare_two(hi, MAX, 1, c)
+            compare_two(lo, MIN, 1, c)
         round_third(1, CHUNK, V)
         for c in range(halves):
             for d in (1, 2):

@@ -183,7 +183,7 @@ def tile_picked_pna_none_p_kernel(
             make_h(t, s)
 
         halves = V // CHUNK
-        g = [[keep.tile([P, 2, V], F32, name=f"g{d}{u}", tag=f"g{d}{u}", align_bytes=64) for u in range(2)] for d in range(3)]
+        g = [[keep.tile([P, 2, V], F32, name=f"g{d}{u}", align_bytes=64) for u in range(2)] for d in range(3)]
         totals = [[bank(f"total{u}{c}", ((5, 6), (7, 3))[u][c]) for c in range(halves)] for u in range(2)]
         back = [bank(f"back{c}", (4, 0)[c]) for c in range(halves)]
         z = [[keep.tile([P, CHUNK * PACK], BF16, name=f"z{c}{d}", align_bytes=64) for d in range(3)] for c in range(halves)]
@@ -213,13 +213,13 @@ def tile_picked_pna_none_p_kernel(
                 )
 
         plans = [
-            [(0, 0, 0, 2, True), (0, 1, 0, 2, False), (1, 0, 0, 2, True), (1, 1, 0, 2, False), (2, 0, 0, 2, True), (2, 1, 0, 2, True)],
+            [(0, 0, 0, 2, True), (0, 1, 0, 2, False), (1, 0, 0, 2, True), (1, 1, 0, 2, False), (2, 0, 0, 2, True), (2, 1, 0, 2, False)],
             [(2, 2, 0, 1, True), (2, 3, 0, 1, True), (0, 2, 0, 2, False), (0, 3, 0, 2, True), (1, 2, 0, 1, False), (1, 3, 0, 1, False), (1, 2, 1, 2, False), (1, 3, 1, 2, False), (2, 2, 1, 2, False), (2, 3, 1, 2, False)],
         ]
         for u, plan in enumerate(plans):
             if u == 1:
                 for t, s in later:
-                    empty_h(t, s, False)
+                    empty_h(t, s, (t, s) in ((2, 1), (3, 0)))
             for i, (d, t, c0, c1, on_vector) in enumerate(plan):
                 gather(d, t, c0, c1, on_vector)
                 for c in range(c0, c1):
@@ -294,19 +294,18 @@ def tile_picked_pna_none_p_kernel(
                 nc.scalar.copy(out=result[:], in_=res[:, 0 : v1 - v0])
             nc.sync.dma_start(out=out[:, CHUNK * c + v0 : CHUNK * c + v1], in_=result[:])
 
-        rounded = [keep.tile([P, V * 2], BF16, name=f"rounded{d}", tag=("rounded0", "g00")[d], align_bytes=64) for d in range(2)]
-        third = keep.tile([P, 2, V * 2], BF16, name="third", tag="g10", align_bytes=64)
+        rounded = [keep.tile([P, V * 2], BF16, name=f"rounded{d}", align_bytes=64) for d in range(2)]
+        third = keep.tile([P, 2, V * 2], BF16, name="third", align_bytes=64)
         round_pair(rounded[0][:], 0, 0, 0, V)
         round_pair(rounded[1][:], 1, 0, 0, V)
         round_pair(third[:, 0, :], 2, 0, 0, V)
         round_pair(third[:, 1, 0 : 2 * CHUNK], 2, 1, 0, CHUNK)
         nc.vector.tensor_tensor(out=hi[:, 0, :], in0=rounded[0][:], in1=rounded[1][:], op=MAX)
         nc.vector.tensor_tensor(out=lo[:, 0, :], in0=rounded[0][:], in1=rounded[1][:], op=MIN)
+        round_third(1, CHUNK, V)
         for c in range(halves):
             compare_two(hi, MAX, 1, c)
             compare_two(lo, MIN, 1, c)
-        round_third(1, CHUNK, V)
-        for c in range(halves):
             for d in (1, 2):
                 compare_third(c, d)
             for d in (1, 2):

@@ -74,10 +74,12 @@ def tile_picked_pna_none_p_kernel(
                 row = SPARE + 16 * z + 4 * q
                 nc.sync.dma_start(out=xs[z][32 * q : 32 * q + 4, :].bitcast(I32), in_=picked[row : row + 4, :].bitcast(I32))
 
-        w_raw1 = [early.tile([P, PACK, H // 2], F32, name=f"w_raw1{i}", offset=(0, 4096 + 1280)[i], align_bytes=64) for i in range(2)]
+        cuts = (0, H // 2, 3 * H // 4, H)
+        w_last = early.tile([P, 2, PACK, H // 4], F32, name="w_last", offset=4096 + 1280, align_bytes=64)
+        w_raw1 = [early.tile([P, PACK, H // 2], F32, name="w_raw10", offset=0, align_bytes=64)[:], w_last[:, 0, :, :], w_last[:, 1, :, :]]
         move_scales(0)
-        for i in range(2):
-            nc.sync.dma_start(out=w_raw1[i][:], in_=w_rows[1][:, :, 256 * i : 256 * (i + 1)])
+        for i in range(3):
+            nc.sync.dma_start(out=w_raw1[i], in_=w_rows[1][:, :, cuts[i] : cuts[i + 1]])
         move_scales(1)
 
         ws2 = early.tile([P, 3 * N], U8, name="ws2", offset=4096 + 768, align_bytes=64)
@@ -103,7 +105,7 @@ def tile_picked_pna_none_p_kernel(
             r0 = m0 if z == 0 else 0
             return (
                 w_bf[z][u][:, :, m0:m1, :].rearrange("p e m j -> p m j e"),
-                raw[:].rearrange("p j (m t) -> p m j t", t=PACK)[:, r0 : r0 + m1 - m0, :, 2 * u : 2 * u + 2],
+                raw.rearrange("p j (m t) -> p m j t", t=PACK)[:, r0 : r0 + m1 - m0, :, 2 * u : 2 * u + 2],
             )
 
         def round_w_scalar(*args):
@@ -119,32 +121,27 @@ def tile_picked_pna_none_p_kernel(
             nc.vector.quantize_mx(out=wq[z][:, cols].bitcast(FP8X4), scales=w_scales(z, t0, t1), in_=flat)
 
         nc.vector.tensor_copy(out=xw[0][:], in_=xw_all[0][:].bitcast(U32).indirect(offs_sb[:]))
-        round_w_scalar(0, 0, w_raw0, 0, P)
-        round_w_scalar(0, 1, w_raw0, 0, P)
+        dst, src = w_views(0, 0, w_raw0[:], 0, P)
+        nc.vector.tensor_copy(out=dst, in_=src)
+        round_w_scalar(0, 1, w_raw0[:], 0, P)
         quantize_w(0, 0, 2)
-        late = [keep.tile([P, BANK], U32, name=f"xw1{i}", tag=("w_bf00", "w_raw0")[i], align_bytes=64) for i in range(2)]
-        nc.vector.tensor_copy(out=late[0][:], in_=xw_all[1][:].bitcast(U32).indirect(offs_sb[:, 0 : BANK // 16]))
         quantize_w(0, 2, 4)
-        nc.vector.tensor_copy(out=late[1][:], in_=xw_all[1][:].bitcast(U32).indirect(offs_sb[:, BANK // 16 : S // 16]))
+        xw.append(keep.tile([P, S], U32, name="xw1", tag="w_bf01", align_bytes=64))
+        nc.vector.tensor_copy(out=xw[1][:], in_=xw_all[1][:].bitcast(U32).indirect(offs_sb[:]))
 
         def words(z, c0, c1):
-            if z == 0:
-                return xw[0][:, c0:c1].bitcast(FP8X4)
-            return late[c0 // BANK][:, c0 % BANK : c0 % BANK + c1 - c0].bitcast(FP8X4)
+            return xw[z][:, c0:c1].bitcast(FP8X4)
 
-        round_w_scalar(1, 0, w_raw1[0], 0, P // 2)
-        round_w_scalar(1, 1, w_raw1[0], 0, P // 2)
-        round_w_scalar(1, 0, w_raw1[1], P // 2, P)
-        dst, src = w_views(1, 1, w_raw1[1], P // 2, P)
-        nc.scalar.activation(out=dst[:, 0 : P // 4], in_=src[:, 0 : P // 4], func=COPY)
+        pieces_w = [(w_raw1[i], cuts[i] // PACK, cuts[i + 1] // PACK) for i in range(3)]
+        for piece in pieces_w:
+            round_w_scalar(1, 0, *piece)
+        dst, src = w_views(1, 1, *pieces_w[0])
         nc.gpsimd.tensor_scalar(
-            out=dst[:, P // 4 : P // 2].rearrange("p m j e -> p e m j"),
-            in0=src[:, P // 4 : P // 2].rearrange("p m j e -> p e m j"),
-            scalar1=1.0,
-            scalar2=0.0,
-            op0=MULT,
-            op1=ADD,
+            out=dst.rearrange("p m j e -> p e m j"), in0=src.rearrange("p m j e -> p e m j"), scalar1=1.0, scalar2=0.0, op0=MULT, op1=ADD
         )
+        dst, src = w_views(1, 1, *pieces_w[1])
+        nc.vector.tensor_copy(out=dst, in_=src)
+        round_w_scalar(1, 1, *pieces_w[2])
         quantize_w(1, 0, 1)
         quantize_w(1, 1, 2)
         quantize_w(1, 2, 4)

@@ -61,8 +61,6 @@ def tile_picked_pna_none_p_kernel(
         nc.sync.dma_start(out=xs_all[SPARE:P, :].bitcast(I32), in_=x_scales.rearrange("z r c -> (z r) c").bitcast(I32))
         nc.sync.dma_start(offs_sb[:], offs)
         load_x(0)
-        for d, pos in enumerate((pos1, pos2, pos3)):
-            nc.sync.dma_start(pos_sb[d][:], pos)
         nc.sync.dma_start(out=w_raw0[:], in_=w_rows[0])
         load_x(1)
 
@@ -81,6 +79,8 @@ def tile_picked_pna_none_p_kernel(
         for i in range(3):
             nc.sync.dma_start(out=w_raw1[i], in_=w_rows[1][:, :, cuts[i] : cuts[i + 1]])
         move_scales(1)
+        for d, pos in enumerate((pos1, pos2, pos3)):
+            nc.sync.dma_start(pos_sb[d][:], pos)
 
         ws2 = early.tile([P, 3 * N], U8, name="ws2", offset=4096 + 768, align_bytes=64)
         nc.gpsimd.memset(ws2[:].bitcast(I32), 0)
@@ -112,6 +112,12 @@ def tile_picked_pna_none_p_kernel(
             dst, src = w_views(*args)
             nc.scalar.activation(out=dst, in_=src, func=COPY)
 
+        def round_w_gpsimd(*args):
+            dst, src = w_views(*args)
+            nc.gpsimd.tensor_scalar(
+                out=dst.rearrange("p m j e -> p e m j"), in0=src.rearrange("p m j e -> p e m j"), scalar1=1.0, scalar2=0.0, op0=MULT, op1=ADD
+            )
+
         def w_scales(z, t0, t1):
             return wsc[z][:, P * t0 : P * t1]
 
@@ -121,9 +127,9 @@ def tile_picked_pna_none_p_kernel(
             nc.vector.quantize_mx(out=wq[z][:, cols].bitcast(FP8X4), scales=w_scales(z, t0, t1), in_=flat)
 
         nc.vector.tensor_copy(out=xw[0][:], in_=xw_all[0][:].bitcast(U32).indirect(offs_sb[:]))
-        dst, src = w_views(0, 0, w_raw0[:], 0, P)
-        nc.vector.tensor_copy(out=dst, in_=src)
-        round_w_scalar(0, 1, w_raw0[:], 0, P)
+        round_w_scalar(0, 0, w_raw0[:], 0, P)
+        round_w_scalar(0, 1, w_raw0[:], 0, P // 2)
+        round_w_gpsimd(0, 1, w_raw0[:], P // 2, P)
         quantize_w(0, 0, 2)
         quantize_w(0, 2, 4)
         xw.append(keep.tile([P, S], U32, name="xw1", tag="w_bf01", align_bytes=64))
@@ -135,12 +141,8 @@ def tile_picked_pna_none_p_kernel(
         pieces_w = [(w_raw1[i], cuts[i] // PACK, cuts[i + 1] // PACK) for i in range(3)]
         for piece in pieces_w:
             round_w_scalar(1, 0, *piece)
-        dst, src = w_views(1, 1, *pieces_w[0])
-        nc.gpsimd.tensor_scalar(
-            out=dst.rearrange("p m j e -> p e m j"), in0=src.rearrange("p m j e -> p e m j"), scalar1=1.0, scalar2=0.0, op0=MULT, op1=ADD
-        )
-        dst, src = w_views(1, 1, *pieces_w[1])
-        nc.vector.tensor_copy(out=dst, in_=src)
+        for piece in pieces_w[:2]:
+            round_w_gpsimd(1, 1, *piece)
         round_w_scalar(1, 1, *pieces_w[2])
         quantize_w(1, 0, 1)
         quantize_w(1, 1, 2)

from contextlib import ExitStack

import concourse.mybir as mybir
from concourse.masks import make_identity

K, T, S, V, H, N = 1024, 2048, 1024, 512, 512, 128
FLOPS = 2 * K * H * S + 3 * 2 * H * N * V

F32 = mybir.dt.float32
BF16 = mybir.dt.bfloat16
I32 = mybir.dt.int32
U32 = mybir.dt.uint32
U16 = mybir.dt.uint16
U8 = mybir.dt.uint8
FP8X4 = mybir.dt.float8_e4m3fn_x4
FP4X4 = mybir.dt.float4_e2m1fn_x4
COPY = mybir.ActivationFunctionType.Copy
MULT = mybir.AluOpType.mult
ADD = mybir.AluOpType.add
MAX = mybir.AluOpType.max
MIN = mybir.AluOpType.min

P = 128
PACK = 4
PASSES = K // (P * PACK)
BANK = 512
CHUNK = 256
SUB = 128
SPARE = 96


def tile_picked_pna_none_p_kernel(
    tc, x_words, x_scales, w1, w2_words, w2_scales, w3_words, w3_scales, w4_words, w4_scales, offs, pos1, pos2, pos3, out
):
    nc = tc.nc
    with ExitStack() as ctx:
        lists = ctx.enter_context(tc.tile_pool(name="lists", bufs=1))
        keep = ctx.enter_context(tc.tile_pool(name="keep", bufs=1))
        early = ctx.enter_context(tc.tile_pool(name="early", bufs=1))
        psum = ctx.enter_context(tc.psum_pool(name="psum", bufs=1))

        def bank(name, index):
            return psum.tile([P, BANK], F32, name=name, tag=f"bank{index}")

        offs_sb = lists.tile([P, S // 16], U16, name="offs_sb")
        pos_sb = [lists.tile([P, V // 16], U16, name=f"pos_sb{d}") for d in range(3)]

        xs_all = early.tile([P, T], U8, name="xs_all", offset=4096 - 256, align_bytes=64)
        nc.gpsimd.memset(xs_all[0:SPARE, :].bitcast(I32), 0)
        xs = [keep.tile([P, S], U8, name=f"xs{z}", align_bytes=64) for z in range(PASSES)]
        for z in range(PASSES):
            nc.vector.memset(xs[z][:].bitcast(I32), 0)

        xw_all = [keep.tile([P, T], I32, name=f"xw_all{z}", align_bytes=64) for z in range(PASSES)]
        w_rows = [w1[512 * z : 512 * (z + 1), :].rearrange("(p j) c -> p j c", j=PACK) for z in range(PASSES)]
        w_raw0 = keep.tile([P, PACK, H], F32, name="w_raw0", tag="w_raw0", align_bytes=64)

        def load_x(z):
            nc.sync.dma_start(out=xw_all[z][:], in_=x_words[z].rearrange("p n t -> p (n t)").bitcast(I32))

        nc.sync.dma_start(out=xs_all[SPARE:P, :].bitcast(I32), in_=x_scales.rearrange("z r c -> (z r) c").bitcast(I32))
        nc.sync.dma_start(offs_sb[:], offs)
        load_x(0)
        nc.sync.dma_start(out=w_raw0[:], in_=w_rows[0])
        load_x(1)

        picked = keep.tile([P, S], U8, name="picked", align_bytes=64)
        nc.vector.tensor_copy(out=picked[:], in_=xs_all[:].indirect(offs_sb[:]))

        def move_scales(z):
            for q in range(4):
                row = SPARE + 16 * z + 4 * q
                nc.sync.dma_start(out=xs[z][32 * q : 32 * q + 4, :].bitcast(I32), in_=picked[row : row + 4, :].bitcast(I32))

        cuts = (0, H // 2, 3 * H // 4, H)
        w_last = early.tile([P, 2, PACK, H // 4], F32, name="w_last", offset=4096 + 1280, align_bytes=64)
        w_raw1 = [early.tile([P, PACK, H // 2], F32, name="w_raw10", offset=0, align_bytes=64)[:], w_last[:, 0, :, :], w_last[:, 1, :, :]]
        move_scales(0)
        for i in range(3):
            nc.sync.dma_start(out=w_raw1[i], in_=w_rows[1][:, :, cuts[i] : cuts[i + 1]])
        move_scales(1)
        for d, pos in enumerate((pos1, pos2, pos3)):
            nc.sync.dma_start(pos_sb[d][:], pos)

        ws2 = early.tile([P, 3 * N], U8, name="ws2", offset=4096 + 768, align_bytes=64)
        nc.gpsimd.memset(ws2[:].bitcast(I32), 0)
        ww2 = [early.tile([P, 2 * N], U8, name=f"ww2{d}", offset=4096 + 256 * d, align_bytes=64) for d in range(3)]
        for d, (words, scales) in enumerate(((w2_words, w2_scales), (w3_words, w3_scales), (w4_words, w4_scales))):
            nc.sync.dma_start(out=ww2[d][:].bitcast(I32), in_=words[0].bitcast(I32))
            for q in range(4):
                nc.sync.dma_start(
                    out=ws2[32 * q : 32 * q + 4, d * N : (d + 1) * N].bitcast(I32),
                    in_=scales[0, 4 * q : 4 * q + 4, :].bitcast(I32),
                )

        ident = keep.tile([P, P], F32, name="ident")
        make_identity(nc, ident[:])

        xw = [keep.tile([P, S], U32, name="xw0", align_bytes=64)]
        w_bf = [[keep.tile([P, 2, P, PACK], BF16, name=f"w_bf{z}{u}", tag=f"w_bf{z}{u}", align_bytes=64) for u in range(2)] for z in range(PASSES)]
        wq = [keep.tile([P, H], U32, name=f"wq{z}", align_bytes=64) for z in range(PASSES)]
        wsc = [keep.tile([P, H], U8, name=f"wsc{z}", align_bytes=64) for z in range(PASSES)]

        def w_views(z, u, raw, m0, m1):
            r0 = m0 if z == 0 else 0
            return (
                w_bf[z][u][:, :, m0:m1, :].rearrange("p e m j -> p m j e"),
                raw.rearrange("p j (m t) -> p m j t", t=PACK)[:, r0 : r0 + m1 - m0, :, 2 * u : 2 * u + 2],
            )

        def round_w_scalar(*args):
            dst, src = w_views(*args)
            nc.scalar.activation(out=dst, in_=src, func=COPY)

        def round_w_gpsimd(*args):
            dst, src = w_views(*args)
            nc.gpsimd.tensor_scalar(
                out=dst.rearrange("p m j e -> p e m j"), in0=src.rearrange("p m j e -> p e m j"), scalar1=1.0, scalar2=0.0, op0=MULT, op1=ADD
            )

        def w_scales(z, t0, t1):
            return wsc[z][:, P * t0 : P * t1]

        def quantize_w(z, t0, t1):
            flat = w_bf[z][t0 // 2][:, t0 % 2 : t0 % 2 + t1 - t0, :, :].rearrange("p e m j -> p (e m j)")
            cols = slice(P * t0, P * t1)
            nc.vector.quantize_mx(out=wq[z][:, cols].bitcast(FP8X4), scales=w_scales(z, t0, t1), in_=flat)

        nc.vector.tensor_copy(out=xw[0][:], in_=xw_all[0][:].bitcast(U32).indirect(offs_sb[:]))
        round_w_scalar(0, 0, w_raw0[:], 0, P)
        round_w_scalar(0, 1, w_raw0[:], 0, P // 2)
        round_w_gpsimd(0, 1, w_raw0[:], P // 2, P)
        quantize_w(0, 0, 2)
        quantize_w(0, 2, 4)
        xw.append(keep.tile([P, S], U32, name="xw1", tag="w_bf01", align_bytes=64))
        nc.vector.tensor_copy(out=xw[1][:], in_=xw_all[1][:].bitcast(U32).indirect(offs_sb[:]))

        def words(z, c0, c1):
            return xw[z][:, c0:c1].bitcast(FP8X4)

        pieces_w = [(w_raw1[i], cuts[i] // PACK, cuts[i + 1] // PACK) for i in range(3)]
        for piece in pieces_w:
            round_w_scalar(1, 0, *piece)
        for piece in pieces_w[:2]:
            round_w_gpsimd(1, 1, *piece)
        round_w_scalar(1, 1, *pieces_w[2])
        quantize_w(1, 0, 1)
        quantize_w(1, 1, 2)
        quantize_w(1, 2, 4)

        h = [keep.tile([P, S], F32, name=f"h{t}", align_bytes=64) for t in range(PACK)]
        banks_of = ((0, 1), (2, 3), (4, 0), (1, 2))

        def h_pass(acc, t, z, s):
            nc.tensor.matmul_mx(
                out=acc[:],
                lhsT=wq[z][:, P * t : P * (t + 1)].bitcast(FP8X4),
                lhsT_scale=w_scales(z, t, t + 1),
                rhs=words(z, BANK * s, BANK * (s + 1)),
                rhs_scale=xs[z][:, BANK * s : BANK * (s + 1)],
                start=(z == 0),
                stop=(z == PASSES - 1),
            )

        accs = {}
        def make_h(t, s):
            accs[t, s] = bank(f"acc{t}{s}", banks_of[t][s])
            for z in range(PASSES):
                h_pass(accs[t, s], t, z, s)

        def empty_h(t, s, on_vector):
            if on_vector:
                nc.vector.tensor_copy(out=h[t][:, BANK * s : BANK * (s + 1)], in_=accs[t, s][:])
            else:
                nc.scalar.copy(out=h[t][:, BANK * s : BANK * (s + 1)], in_=accs[t, s][:])

        for t, s in ((0, 0), (0, 1), (1, 0), (1, 1)):
            make_h(t, s)
            empty_h(t, s, s == 0)
        later = [(t, s) for t in (2, 3) for s in range(2)]
        for t, s in later:
            make_h(t, s)

        halves = V // CHUNK
        g = [[keep.tile([P, 2, V], F32, name=f"g{d}{u}", align_bytes=64) for u in range(2)] for d in range(3)]
        totals = [[bank(f"total{u}{c}", ((5, 6), (7, 3))[u][c]) for c in range(halves)] for u in range(2)]
        back = [bank(f"back{c}", (4, 0)[c]) for c in range(halves)]
        z = [[keep.tile([P, CHUNK * PACK], BF16, name=f"z{c}{d}", align_bytes=64) for d in range(3)] for c in range(halves)]
        hi = keep.tile([P, 2, V * 2], BF16, name="hi", align_bytes=64)
        lo = keep.tile([P, 2, V * 2], BF16, name="lo", align_bytes=64)

        def gather(d, t, c0, c1, on_vector):
            u, e = divmod(t, 2)
            window = h[t][:].indirect(pos_sb[d][:, CHUNK // 16 * c0 : CHUNK // 16 * c1])
            if on_vector:
                nc.vector.tensor_copy(out=g[d][u][:, e, CHUNK * c0 : CHUNK * c1], in_=window)
            else:
                nc.scalar.activation(out=g[d][u][:, e, CHUNK * c0 : CHUNK * c1], in_=window, func=COPY)

        def add_up(d, t, c, first, last):
            u, e = divmod(t, 2)
            for s in range(2):
                v0 = CHUNK * c + SUB * s
                col = P * (2 * s + e)
                nc.tensor.matmul(
                    totals[u][c][:, col : col + P],
                    lhsT=g[d][u][:, e, v0 : v0 + SUB],
                    rhs=ident[:],
                    is_transpose=True,
                    start=(first and s == 0),
                    stop=(last and s == 1),
                )

        plans = [
            [(0, 0, 0, 2, True), (0, 1, 0, 2, False), (1, 0, 0, 2, True), (1, 1, 0, 2, False), (2, 0, 0, 2, True), (2, 1, 0, 2, False)],
            [(2, 2, 0, 1, True), (2, 3, 0, 1, True), (0, 2, 0, 2, False), (0, 3, 0, 2, True), (1, 2, 0, 1, False), (1, 3, 0, 1, False), (1, 2, 1, 2, False), (1, 3, 1, 2, False), (2, 2, 1, 2, False), (2, 3, 1, 2, False)],
        ]
        for u, plan in enumerate(plans):
            if u == 1:
                for t, s in later:
                    empty_h(t, s, (t, s) in ((2, 1), (3, 0)))
            for i, (d, t, c0, c1, on_vector) in enumerate(plan):
                gather(d, t, c0, c1, on_vector)
                for c in range(c0, c1):
                    steps = [j for j, step in enumerate(plan) if step[2] <= c < step[3]]
                    add_up(d, t, c, i == steps[0], i == steps[-1])

        def by_rows(d, u, v0, v1):
            return g[d][u][:, :, v0:v1].rearrange("p e (v i) -> p v e i", i=4)

        def paired(tile, u, v0, v1):
            return tile[:, u, 2 * v0 : 2 * v1].rearrange("p (v i e) -> p v e i", i=4, e=2)

        def woven(tile, c):
            return tile[:, :, CHUNK * 2 * c : CHUNK * 2 * (c + 1)].rearrange("p u (v e) -> p v u e", e=2)

        def turn(u, c):
            turned = keep.tile([P, 2 * P * 2], BF16, name=f"turned{u}{c}", align_bytes=64)
            nc.scalar.activation(
                out=turned[:].rearrange("v (s p e) -> v s p e", s=2, e=2),
                in_=totals[u][c][:].rearrange("v (s e p) -> v s p e", s=2, e=2),
                func=COPY,
                scale=1.0 / 3.0,
            )
            pairs = turned[:].bitcast(F32)
            for s in range(2):
                nc.tensor.transpose(back[c][:, P * (2 * s + u) : P * (2 * s + u + 1)], pairs[:, P * s : P * (s + 1)], ident[:])

        def weave(c, s0, s1):
            nc.scalar.copy(
                out=z[c][0][:, PACK * SUB * s0 : PACK * SUB * s1].bitcast(F32).rearrange("p (s v u) -> p s v u", v=SUB, u=2),
                in_=back[c][:, 2 * SUB * s0 : 2 * SUB * s1].rearrange("p (s u v) -> p s v u", v=SUB, u=2),
            )

        def compare_two(tile, op, u, c):
            v0, v1 = CHUNK * c, CHUNK * (c + 1)
            nc.vector.tensor_tensor(out=paired(tile, u, v0, v1), in0=by_rows(0, u, v0, v1), in1=by_rows(1, u, v0, v1), op=op)

        def round_third(u, v0, v1):
            nc.scalar.copy(out=paired(third, u, v0, v1), in_=by_rows(2, u, v0, v1))

        def round_pair(dst, d, u, v0, v1):
            nc.gpsimd.tensor_scalar(
                out=dst.rearrange("p (v e) -> p v e", e=2), in0=g[d][u][:, :, v0:v1].rearrange("p e v -> p v e"), scalar1=1.0, scalar2=0.0, op0=MULT, op1=ADD
            )

        def compare_third(c, d):
            tile, op = ((hi, MAX), (lo, MIN))[d - 1]
            nc.vector.tensor_tensor(out=z[c][d][:].rearrange("p (v u e) -> p v u e", u=2, e=2), in0=woven(tile, c), in1=woven(third, c), op=op)

        zq = [[keep.tile([P, CHUNK], U32, name=f"zq{c}{d}", align_bytes=64) for d in range(3)] for c in range(halves)]
        zs = [[keep.tile([P, CHUNK], U8, name=f"zs{c}{d}", align_bytes=64) for d in range(3)] for c in range(halves)]

        def quantize_z(c, d, v0, v1):
            nc.vector.quantize_mx(out=zq[c][d][:, v0:v1].bitcast(FP8X4), scales=zs[c][d][:, v0:v1], in_=z[c][d][:, PACK * v0 : PACK * v1])

        def product(res, c, d, v0, v1):
            nc.tensor.matmul_mx(
                out=res[:, 0 : v1 - v0],
                lhsT=ww2[d][:].bitcast(FP4X4),
                lhsT_scale=ws2[:, d * N : (d + 1) * N],
                rhs=zq[c][d][:, v0:v1].bitcast(FP8X4),
                rhs_scale=zs[c][d][:, v0:v1],
                start=(d == 1),
                stop=(d == 0),
            )

        def store(res, c, v0, v1, on_vector):
            result = keep.tile([P, v1 - v0], F32, name=f"result{c}{v0}")
            if on_vector:
                nc.vector.tensor_copy(out=result[:], in_=res[:, 0 : v1 - v0])
            else:
                nc.scalar.copy(out=result[:], in_=res[:, 0 : v1 - v0])
            nc.sync.dma_start(out=out[:, CHUNK * c + v0 : CHUNK * c + v1], in_=result[:])

        rounded = [keep.tile([P, V * 2], BF16, name=f"rounded{d}", align_bytes=64) for d in range(2)]
        third = keep.tile([P, 2, V * 2], BF16, name="third", align_bytes=64)
        round_pair(rounded[0][:], 0, 0, 0, V)
        round_pair(rounded[1][:], 1, 0, 0, V)
        round_pair(third[:, 0, :], 2, 0, 0, V)
        round_pair(third[:, 1, 0 : 2 * CHUNK], 2, 1, 0, CHUNK)
        nc.vector.tensor_tensor(out=hi[:, 0, :], in0=rounded[0][:], in1=rounded[1][:], op=MAX)
        nc.vector.tensor_tensor(out=lo[:, 0, :], in0=rounded[0][:], in1=rounded[1][:], op=MIN)
        round_third(1, CHUNK, V)
        for c in range(halves):
            compare_two(hi, MAX, 1, c)
            compare_two(lo, MIN, 1, c)
            for d in (1, 2):
                compare_third(c, d)
            for d in (1, 2):
                quantize_z(c, d, 0, CHUNK)
        for u in range(2):
            for c in range(halves):
                turn(u, c)
        weave(0, 0, 2)
        weave(1, 0, 1)
        weave(1, 1, 2)
        pieces = [(bank("res0", 1), 0, 0, CHUNK), (bank("res1", 2), 1, 0, SUB), (bank("res2", 5), 1, SUB, CHUNK)]
        for res, c, v0, v1 in pieces:
            for d in (1, 2):
                product(res, c, d, v0, v1)
        for i, (res, c, v0, v1) in enumerate(pieces):
            quantize_z(c, 0, v0, v1)
            product(res, c, 0, v0, v1)
            store(res, c, v0, v1, i == len(pieces) - 1)
